import numpy as np
import ml_dtypes


def mxq(x, axis, fmt="e4m3"):
    dtype, down = {"e4m3": (ml_dtypes.float8_e4m3fn, 7), "e5m2": (ml_dtypes.float8_e5m2, 14)}[fmt]
    v = np.moveaxis(np.asarray(x, np.float32).astype(ml_dtypes.bfloat16).astype(np.float64), axis, -1)
    blocks = v.reshape(v.shape[:-1] + (-1, 32))
    amax = np.abs(blocks).max(-1, keepdims=True)
    byte = np.maximum(np.where(amax > 0, np.frexp(amax)[1] - 1 + 127, 0) - down, 1)
    scale = np.exp2(byte - 127.0)
    codes = (blocks / scale).astype(np.float32).astype(dtype).astype(np.float64)
    return np.moveaxis((codes * scale).reshape(v.shape), -1, axis)


WIDE = False


def mx_kscale(k):
    if not WIDE:
        return np.ones(k)
    levels = np.array([30, -30])
    if k % 512:
        return np.exp2(np.random.permutation(np.resize(levels, k // 32))).repeat(32)
    a = np.empty((k // 512, 16))
    for p in range(k // 512):
        a[p, :8] = np.random.permutation(np.resize(levels, 8))
        for g in range(8):
            far = levels[np.abs(levels - a[p, g]) >= 10]
            a[p, g + 8] = far[np.random.randint(len(far))]
    return np.exp2(a.ravel()).repeat(32)


BF16 = ml_dtypes.bfloat16


def bf(x):
    return np.asarray(x, np.float32).astype(BF16)


def f64(x):
    return np.asarray(x).astype(np.float64)


E2M1 = np.array([0.0, 0.5, 1.0, 1.5, 2.0, 3.0, 4.0, 6.0, -0.0, -0.5, -1.0, -1.5, -2.0, -3.0, -4.0, -6.0])


def pack_weight(w, fmt):
    k, n = w.shape
    w = f64(bf(w)).reshape(k // 32, 32, n)
    amax = np.abs(w).max(1)
    if fmt in ("e4m3", "e5m2"):
        byte = np.frexp(amax)[1] - 1 + 127 - (7 if fmt == "e4m3" else 14)
    else:
        mant, ex = np.frexp(amax / 6.0)
        byte = np.where(mant > 0.5, ex, ex - 1) + 127
    byte = np.clip(np.where(amax > 0, byte, 1), 1, 254)
    scaled = (w * np.exp2(127.0 - byte)[:, None, :]).reshape(k, n).astype(np.float32)
    by_word = np.ascontiguousarray(scaled.reshape(k // 512, 128, 4, n).transpose(0, 1, 3, 2))
    if fmt in ("e4m3", "e5m2"):
        words = by_word.astype(ml_dtypes.float8_e4m3fn if fmt == "e4m3" else ml_dtypes.float8_e5m2).view(np.uint8)
    else:
        c = by_word.astype(ml_dtypes.float4_e2m1fn).view(np.uint8) & 0xF
        words = c[..., 0::2] | (c[..., 1::2] << 4)
    return np.ascontiguousarray(words), np.ascontiguousarray(byte.astype(np.uint8).reshape(k // 512, 16, n))


def unpack_weight(words, scales, fmt):
    g, p, n, _ = words.shape
    if fmt in ("e4m3", "e5m2"):
        vals = np.ascontiguousarray(words).view(ml_dtypes.float8_e4m3fn if fmt == "e4m3" else ml_dtypes.float8_e5m2).astype(np.float64)
    else:
        nib = np.empty((g, p, n, 4), np.uint8)
        nib[..., 0::2] = words & 0xF
        nib[..., 1::2] = words >> 4
        vals = E2M1[nib]
    vals = vals * np.repeat(np.exp2(scales.astype(np.float64) - 127.0), 8, axis=1)[..., None]
    return vals.transpose(0, 1, 3, 2).reshape(g * 512, n)

def planes(Y):
    n, m = Y.shape
    b = f64(bf(Y)).reshape(n // 32, 32, m)
    amax = np.abs(b).max(1)
    byte = np.clip(np.where(amax > 0, np.frexp(amax)[1] - 1 + 127 - 7, 1), 1, 254)
    codes = (b * np.exp2(127.0 - byte)[:, None, :]).reshape(n, m).astype(np.float32).astype(ml_dtypes.float8_e4m3fn).view(np.uint8)
    words = codes.reshape(n // 512, 128, 4, m).transpose(0, 1, 3, 2)
    return np.ascontiguousarray(words), np.ascontiguousarray(byte.astype(np.uint8).reshape(n // 512, 16, m))


R, K, C, D = 1536, 2048, 1024, 3
SOFT = 0.1

def dipole_kernel(pos, normal, query):
    d = pos[:, None, :] - query[None, :, :]
    dist2 = (d * d).sum(-1) + SOFT ** 2
    return (normal[:, None, :] * d).sum(-1) / dist2 ** 1.5

def setup_inputs():
    s = mx_kscale(K)
    u = np.random.randn(K, D)
    u = u / np.sqrt((u * u).sum(-1, keepdims=True))
    pos = u * (1.0 + 0.1 * np.random.randn(K, 1))
    normal = u + 0.2 * np.random.randn(K, D)
    normal = normal / np.sqrt((normal * normal).sum(-1, keepdims=True))
    query = 0.7 * np.random.randn(R, D)
    G = dipole_kernel(pos, normal, query) / np.sqrt(K)
    g_words, g_scales = pack_weight(G * s[:, None], "e5m2")
    density = bf(np.random.randn(K, C) / s[:, None])
    area_weight = bf(np.exp(0.4 * np.random.randn(K)))
    spread = np.exp(0.8 * np.random.randn(C))
    gain = bf(spread)
    field = bf(0.5 * np.random.randn(R, C) * spread)
    return {"g_words": g_words, "g_scales": g_scales, "density": density,
            "area_weight": area_weight, "gain": gain, "field": field}

def reference(g_words, g_scales, density, area_weight, gain, field):
    G = unpack_weight(g_words, g_scales, "e5m2")
    A = f64(area_weight)[:, None] * f64(density)
    U = G.T @ mxq(A, 0, "e4m3")
    y = f64(field) + U * f64(gain)[None, :]
    Y = y.T
    words, scales = planes(Y)
    return y, words, scales

@@ -1,0 +1,361 @@
+from contextlib import ExitStack
+
+import concourse.mybir as mybir
+from concourse.masks import make_identity
+
+F32 = mybir.dt.float32
+BF16 = mybir.dt.bfloat16
+I32 = mybir.dt.int32
+U32 = mybir.dt.uint32
+U8 = mybir.dt.uint8
+E4M3 = mybir.dt.float8_e4m3fn_x4
+E5M2 = mybir.dt.float8_e5m2_x4
+MULT = mybir.AluOpType.mult
+ADD = mybir.AluOpType.add
+
+R, K, C = 1536, 2048, 1024
+FLOPS = 2 * R * K * C
+P = 128
+PACK = 4
+KP = P * PACK
+N = 512
+GROUPS = K // KP
+HALVES = C // N
+UNITS = GROUPS * HALVES
+RT = R // P
+TILES = RT * HALVES
+PAIRS = TILES // 2
+Y16_BUFS = 12
+YT_BUFS = 6
+
+
+def needs(step, loads):
+    kind = step[0]
+    if kind in ("gs", "ones", "gain"):
+        return [("init",)]
+    if kind == "gmm":
+        return [("ones",), ("gain",)]
+    if kind == "gb":
+        return [("gmm",)]
+    if kind == "cmm":
+        return [("ones",), ("gain",)]
+    if kind == "cb":
+        return [("cmm",)]
+    if kind == "zc":
+        n = step[1]
+        j = C_CHUNKS.index(n // 4)
+        old = [("tc", 4 * C_CHUNKS[j - ZT_BUFS] + a) for a in range(4)] if j >= ZT_BUFS else []
+        return [("mx", n, GROUPS - 1), ("cb",)] + old
+    if kind == "tc":
+        n = step[1]
+        return [("zc", n - n % 4 + ct) for ct in range(4)] + [("ident",)] + t_bank_free(step)
+    if kind == "m":
+        return [("d", step[1]), ("area",)]
+    if kind in ("iv", "is"):
+        return [("m", step[1])] + ([("q", step[1] - GROUPS)] if step[1] >= GROUPS else [])
+    if kind == "q":
+        u = step[1]
+        return ([("iv", u)] if V_COLS[u] > 0 else []) + ([("is", u)] if V_COLS[u] < N else [])
+    if kind == "mx":
+        n, g = step[1:]
+        h, rt = divmod(n, RT)
+        out = [("q", h * GROUPS + g)] + [("gs", q) for q in range(4)]
+        rts = range(rt - rt % 4, rt - rt % 4 + 4) if n // 4 in C_CHUNKS else [rt]
+        out += [s for s in loads if s[0] == "G" and s[1] <= g < s[2] and any(s[3] <= x < s[4] for x in rts)]
+        if g > 0:
+            out.append(("mx", n, g - 1))
+        elif n >= MX_BANKS:
+            out.append(scale_step(n - MX_BANKS))
+        return out
+    if kind == "z":
+        return [("mx", step[1], GROUPS - 1), ("gb",)]
+    if kind in ("y", "yg", "yb"):
+        n = step[1]
+        out = [("tc" if n // 4 in C_CHUNKS else "z", n)] + [s for s in loads if s[0] == "f" and s[1] <= n < s[2]]
+        if kind == "yb":
+            return out + [("t", turn_of(n - Y16_BUFS))]
+        return out + ([("yb", n)] if n in V_CAST else [])
+    if kind in ("c", "cg"):
+        n = step[1]
+        return [add_step(n)] + ([("t", turn_of(n - Y16_BUFS))] if n >= Y16_BUFS else [])
+    if kind == "t":
+        k = step[1]
+        return [cast_step(n) for n in range(*TURNS[k])] + [("ident",)] + t_bank_free(step)
+    if kind == "p":
+        return [("t", step[1])] + ([("qy", step[1] - YT_BUFS)] if step[1] >= YT_BUFS else [])
+    if kind == "qy":
+        return [("p", step[1])]
+    if kind == "sy":
+        return [add_step(n) for n in range(step[1], step[2])]
+    if kind == "sw":
+        return [("qy", turn_of(n)) for n in range(step[1], step[2])]
+    if kind in ("ss", "ss2"):
+        return [("qy", turn_of(n)) for n in range(step[1] * RT, (step[1] + 1) * RT)]
+    return []
+
+
+def turn_of(n):
+    return [k for k, (n0, n1) in enumerate(TURNS) if n0 <= n < n1][0]
+
+
+def scale_step(n):
+    return ("zc" if n // 4 in C_CHUNKS else "z", n)
+
+
+def t_bank_free(step):
+    i = T_USES.index(step)
+    if i < T_BANKS:
+        return [("gb",)] + ([("cb",)] if C_CHUNKS else [])
+    kind, k = T_USES[i - T_BANKS]
+    return [("p", k) if kind == "t" else ("y", k)]
+
+
+def add_step(n):
+    return ("yg" if n in G_ADD else "y", n)
+
+
+def cast_step(n):
+    return ("cg" if n in G_CAST else "yb" if n in V_CAST else "c", n)
+
+
+V_COLS = [256,256,256,128,128,0,0,0]
+G_ADD = ()
+G_CAST = ()
+V_CAST = (23,)
+C_CHUNKS = []
+MX_BANKS = 6
+T_BANKS = 2
+ZT_BUFS = 1
+TURNS = [(n, n + 2) for n in range(0, 22, 2)] + [(22, 23), (23, 24)]
+T_USES = [("t", k) for k in range(len(TURNS))]
+LOADS = (
+    [("area",), ("d", 0), ("d", 1), ("gain",), ("d", 2), ("d", 3)] + [("gs", q) for q in range(4)]
+    + [("G", 0, 2, 0, 4), ("d", 4), ("G", 2, 4, 0, 4), ("d", 5), ("G", 0, 4, 4, 6), ("d", 6),
+       ("G", 0, 4, 6, 8), ("G", 0, 4, 8, 12), ("d", 7), ("f", 0, 4), ("f", 4, 8), ("f", 8, 12), ("f", 12, 18), ("f", 18, 24)]
+)
+
+
+def engine_orders():
+    sync = list(LOADS)
+    sync += [("sy", 0, 4), ("sy", 4, 8), ("sy", 8, 12), ("sw", 0, 6), ("sy", 12, 16), ("sw", 6, 12)] + [("ss", 0, q) for q in range(4)] + [("sy", 16, 18), ("sy", 18, 20), ("sw", 12, 16), ("sy", 20, 22), ("sy", 22, 23), ("sw", 16, 20), ("sy", 23, 24), ("sw", 20, 24), ("ss", 1, 0), ("ss", 1, 1)]
+
+    vec = [("init",), ("m", 0)]
+    for u in range(1, 6):
+        vec += [("iv", u - 1), ("m", u), ("q", u - 1)]
+    vec = [s for s in vec if s[0] != "iv" or V_COLS[s[1]]]
+    vec += [("z", 0), ("z", 1), ("z", 2), ("m", 6), ("z", 3), ("z", 4), ("q", 5), ("z", 5), ("z", 6), ("m", 7), ("q", 6), ("z", 7), ("y", 0), ("y", 1), ("z", 8), ("q", 7)]
+    zs = [n for n in range(TILES) if ("z", n) not in vec]
+    ys = [n for n in range(TILES - 1) if ("y", n) not in vec]
+    k = 0
+    while ys:
+        if zs:
+            vec.append(("z", zs.pop(0)))
+        for i in range(2 if len(ys) > len(zs) + 1 else 1):
+            n = ys.pop(0)
+            vec.append(("y", n))
+            if n % 2 == 1 and n >= 7:
+                vec.append(("qy", k))
+                k += 1
+    vec.insert(vec.index(("y", TILES - 2)), ("yb", TILES - 1))
+    vec.insert(vec.index(("y", TILES - 2)) + 1, ("y", TILES - 1))
+    vec += [("qy", j) for j in range(k, len(TURNS))]
+
+    act = [("ones",)] + [("is", u) for u in range(4)] + [("gb",)]
+    act += [("is", u) for u in range(4, 8)]
+    act = [s for s in act if s[0] != "is" or V_COLS[s[1]] < N]
+    for k in range(PAIRS - 1):
+        act += [("c", 2 * k), ("c", 2 * k + 1)] + ([("p", k - 1)] if k >= 1 else [])
+    act += [("c", 22)] + [("p", k) for k in range(PAIRS - 1 - 1, len(TURNS))] + [("ss2", 1, 2), ("ss2", 1, 3)]
+
+    pe = [("gmm",)] + [("mx", n, g) for g in range(GROUPS) for n in range(4)]
+    pe += [("mx", n, g) for n in range(4, 15) for g in range(GROUPS)]
+    k = 0
+    for n in range(15, TILES, 2):
+        pe += [("t", k), ("t", k + 1)] + [("mx", i, g) for i in range(n, min(n + 2, TILES)) for g in range(GROUPS)]
+        k += 2
+    pe += [("t", j) for j in range(k, len(TURNS))]
+    return [sync, vec, act, pe, [("ident",)]]
+
+
+def tile_winding_dipole_sum_k2_kernel(
+    tc, g_words, g_scales, density, area_weight, gain, field, out_0, out_1, out_2
+):
+    nc = tc.nc
+    with ExitStack() as ctx:
+        sb = ctx.enter_context(tc.tile_pool(name="sb", bufs=1))
+        ps = ctx.enter_context(tc.psum_pool(name="ps", bufs=1))
+
+        area = sb.tile([P, GROUPS, PACK], BF16)
+        gain_row = sb.tile([P, C], BF16)
+        gain_all = sb.tile([P, C], BF16)
+        ones_f32 = sb.tile([P, P], F32)
+        ones = sb.tile([P, P], BF16)
+        ident = sb.tile([P, P], F32)
+        gw = sb.tile([P, GROUPS, R], U32, align_bytes=64)
+        gs = sb.tile([P, GROUPS, R], U8, align_bytes=64)
+        rows = sb.tile([P, UNITS, PACK, N], BF16, align_bytes=64)
+        packed = sb.tile([P, GROUPS, N, PACK], BF16, align_bytes=64)
+        aw = sb.tile([P, UNITS, N], U32, align_bytes=64)
+        asc = sb.tile([P, UNITS, N], U8, align_bytes=64)
+        fld = sb.tile([P, TILES, N], BF16, align_bytes=64)
+        y = sb.tile([P, TILES, N], F32, align_bytes=64)
+        y16 = sb.tile([P, Y16_BUFS, N], BF16, align_bytes=64)
+        yt = sb.tile([P, YT_BUFS, 2 * P, PACK], BF16, align_bytes=64)
+        yw = sb.tile([P, HALVES, R], U32, align_bytes=64)
+        ysc = sb.tile([P, HALVES, R], U8, align_bytes=64)
+        banks = [ps.tile([P, N], F32, name="bank%d" % i) for i in range(8)]
+
+        g_src = g_words.rearrange("g p n t -> p g (n t)")
+        w_dst = out_1.rearrange("g p m t -> p g (m t)")
+
+        def hbm_tiles(ap, n0, n1):
+            h, r0 = divmod(n0, RT)
+            part = ap[r0 * P : (r0 + n1 - n0) * P, h * N : (h + 1) * N]
+            return part.rearrange("(a p) c -> p a c", p=P)
+
+        def run(step):
+            kind = step[0]
+            if kind == "init":
+                nc.vector.memset(ones_f32[:], 1.0)
+                nc.vector.memset(gain_row[:], 0.0)
+                nc.vector.memset(gs[:].rearrange("p g n -> p (g n)").bitcast(U32), 0)
+            elif kind == "ident":
+                make_identity(nc, ident[:])
+            elif kind == "area":
+                nc.sync.dma_start(out=area[:], in_=area_weight.rearrange("(g p t) -> p g t", p=P, t=PACK))
+            elif kind == "ones":
+                nc.scalar.copy(out=ones[:], in_=ones_f32[:])
+            elif kind == "gain":
+                nc.sync.dma_start(out=gain_row[0:1, :], in_=gain.rearrange("(o c) -> o c", o=1))
+            elif kind == "gmm":
+                for h in range(HALVES):
+                    nc.tensor.matmul(
+                        out=banks[7][:].bitcast(BF16)[:, h * N : (h + 1) * N],
+                        lhsT=ones[:], rhs=gain_row[:, h * N : (h + 1) * N], start=True, stop=True,
+                    )
+            elif kind == "gb":
+                nc.scalar.copy(out=gain_all[:], in_=banks[7][:].bitcast(BF16))
+            elif kind == "d":
+                h, g = divmod(step[1], GROUPS)
+                src = density[g * KP : (g + 1) * KP, h * N : (h + 1) * N]
+                nc.sync.dma_start(out=rows[:, step[1]], in_=src.rearrange("(p t) c -> p t c", t=PACK))
+            elif kind == "gs":
+                q = step[1]
+                nc.sync.dma_start(
+                    out=gs[32 * q : 32 * q + 4].bitcast(I32),
+                    in_=g_scales[:, 4 * q : 4 * q + 4, :].rearrange("g j n -> j g n").bitcast(I32),
+                )
+            elif kind == "G":
+                g0, g1, r0, r1 = step[1:]
+                nc.sync.dma_start(
+                    out=gw[:, g0:g1, r0 * P : r1 * P].bitcast(I32),
+                    in_=g_src[:, g0:g1, r0 * P * PACK : r1 * P * PACK].bitcast(I32),
+                )
+            elif kind == "f":
+                nc.sync.dma_start(out=fld[:, step[1] : step[2]], in_=hbm_tiles(field, step[1], step[2]))
+            elif kind == "m":
+                u = step[1]
+                for t in range(PACK):
+                    nc.vector.tensor_scalar(
+                        out=rows[:, u, t], in0=rows[:, u, t], scalar1=area[:, u % GROUPS, t : t + 1],
+                        scalar2=None, op0=MULT,
+                    )
+            elif kind in ("iv", "is"):
+                u = step[1]
+                cols = slice(0, V_COLS[u]) if kind == "iv" else slice(V_COLS[u], N)
+                dst = packed[:, u % GROUPS, cols].rearrange("p (c i) t -> p c t i", i=4)
+                src = rows[:, u, :, cols].rearrange("p t (c i) -> p c t i", i=4)
+                if kind == "iv":
+                    nc.vector.tensor_copy(out=dst, in_=src)
+                else:
+                    nc.scalar.copy(out=dst, in_=src)
+            elif kind == "q":
+                u = step[1]
+                nc.vector.quantize_mx(
+                    out=aw[:, u].bitcast(E4M3), scales=asc[:, u],
+                    in_=packed[:, u % GROUPS].rearrange("p c t -> p (c t)"),
+                )
+            elif kind == "mx":
+                n, g = step[1:]
+                h, rt = divmod(n, RT)
+                cols = slice(rt * P, (rt + 1) * P)
+                nc.tensor.matmul_mx(
+                    out=banks[n % MX_BANKS][:],
+                    lhsT=gw[:, g, cols].bitcast(E5M2), lhsT_scale=gs[:, g, cols],
+                    rhs=aw[:, h * GROUPS + g].bitcast(E4M3), rhs_scale=asc[:, h * GROUPS + g],
+                    start=(g == 0), stop=(g == GROUPS - 1),
+                )
+            elif kind == "z":
+                n = step[1]
+                h = n // RT
+                nc.vector.tensor_tensor(
+                    out=y[:, n], in0=banks[n % MX_BANKS][:], in1=gain_all[:, h * N : (h + 1) * N], op=MULT
+                )
+            elif kind in ("y", "yg"):
+                n = step[1]
+                eng = nc.vector if kind == "y" else nc.gpsimd
+                eng.tensor_tensor(out=y[:, n], in0=y[:, n], in1=fld[:, n], op=ADD)
+            elif kind in ("c", "cg"):
+                n = step[1]
+                dst = y16[:, n % Y16_BUFS].rearrange("r (u p e) -> r u p e", u=2, e=2)
+                src = y[:, n].rearrange("r (p u e) -> r u p e", u=2, e=2)
+                if kind == "c":
+                    nc.scalar.copy(out=dst, in_=src)
+                else:
+                    nc.gpsimd.tensor_scalar(out=dst, in0=src, scalar1=1.0, scalar2=-0.0, op0=MULT, op1=ADD)
+            elif kind == "yb":
+                n = step[1]
+                order = "r (p u e) -> r u p e"
+                nc.vector.tensor_tensor(
+                    out=y16[:, n % Y16_BUFS].rearrange("r (u p e) -> r u p e", u=2, e=2),
+                    in0=y[:, n].rearrange(order, u=2, e=2), in1=fld[:, n].rearrange(order, u=2, e=2), op=ADD,
+                )
+            elif kind == "t":
+                n0, n1 = TURNS[step[1]]
+                w = (n1 - n0) * P
+                bank = banks[MX_BANKS + step[1] % T_BANKS][:, : 2 * w].rearrange("p (u r) -> p u r", u=2)
+                for j in range(n1 - n0):
+                    words = y16[:, (n0 + j) % Y16_BUFS].bitcast(F32)
+                    for u in range(2):
+                        nc.tensor.transpose(bank[:, u, j * P : (j + 1) * P], words[:, u * P : (u + 1) * P], ident[:])
+            elif kind == "p":
+                n0, n1 = TURNS[step[1]]
+                w = (n1 - n0) * P
+                bank = banks[MX_BANKS + step[1] % T_BANKS][:, : 2 * w].rearrange("p (u r) -> p r u", u=2)
+                dst = yt[:, step[1] % YT_BUFS, :w].rearrange("p r t -> p (r t)").bitcast(F32)
+                nc.scalar.copy(out=dst.rearrange("p (r u) -> p r u", u=2), in_=bank)
+            elif kind == "qy":
+                n0, n1 = TURNS[step[1]]
+                h, rt = divmod(n0, RT)
+                cols = slice(rt * P, (rt + n1 - n0) * P)
+                nc.vector.quantize_mx(
+                    out=yw[:, h, cols].bitcast(E4M3), scales=ysc[:, h, cols],
+                    in_=yt[:, step[1] % YT_BUFS, : (n1 - n0) * P].rearrange("p r t -> p (r t)"),
+                )
+            elif kind == "sy":
+                nc.sync.dma_start(out=hbm_tiles(out_0, step[1], step[2]), in_=y[:, step[1] : step[2]])
+            elif kind == "sw":
+                h, rt = divmod(step[1], RT)
+                r0, r1 = rt * P, (rt + step[2] - step[1]) * P
+                nc.sync.dma_start(
+                    out=w_dst[:, h, r0 * PACK : r1 * PACK].bitcast(I32), in_=yw[:, h, r0:r1].bitcast(I32)
+                )
+            elif kind in ("ss", "ss2"):
+                h, q = step[1:]
+                eng = nc.sync if kind == "ss" else nc.scalar
+                eng.dma_start(
+                    out=out_2[h, 4 * q : 4 * q + 4, :].bitcast(I32), in_=ysc[32 * q : 32 * q + 4, h].bitcast(I32)
+                )
+
+        queues = engine_orders()
+        done = set()
+        with tc.manual_schedule():
+            while any(queues):
+                moved = False
+                for queue in queues:
+                    while queue and all(need in done for need in needs(queue[0], LOADS)):
+                        step = queue.pop(0)
+                        run(step)
+                        done.add(step)
+                        moved = True
+                assert moved

@@ -21,15 +21,23 @@ KP = P * PACK
 N = 512
 GROUPS = K // KP
 HALVES = C // N
-UNITS = GROUPS * HALVES
 RT = R // P
-TILES = RT * HALVES
-PAIRS = TILES // 2
-Y16_BUFS = 12
-YT_BUFS = 6
+SUMS = RT * HALVES
+BANKS = 8
+MX_BANKS = 6
+Y16_BUFS = 6
+CHUNK = 4
 
 
-def needs(step, loads):
+def sum_bank(n):
+    return n if n < BANKS else (n - BANKS) % MX_BANKS
+
+
+def covering(steps, kind, rt, h):
+    return [s for s in steps if s[0] in kind and s[1] == rt and s[2] < (h + 1) * N and s[3] > h * N]
+
+
+def needs(step, plan):
     kind = step[0]
     if kind in ("gs", "ones", "gain"):
         return [("init",)]
@@ -37,144 +45,100 @@ def needs(step, loads):
         return [("ones",), ("gain",)]
     if kind == "gb":
         return [("gmm",)]
-    if kind == "cmm":
-        return [("ones",), ("gain",)]
-    if kind == "cb":
-        return [("cmm",)]
-    if kind == "zc":
-        n = step[1]
-        j = C_CHUNKS.index(n // 4)
-        old = [("tc", 4 * C_CHUNKS[j - ZT_BUFS] + a) for a in range(4)] if j >= ZT_BUFS else []
-        return [("mx", n, GROUPS - 1), ("cb",)] + old
-    if kind == "tc":
-        n = step[1]
-        return [("zc", n - n % 4 + ct) for ct in range(4)] + [("ident",)] + t_bank_free(step)
     if kind == "m":
-        return [("d", step[1]), ("area",)]
+        g, c0, c1 = step[1:]
+        return [("area",)] + [s for s in plan if s[0] == "d" and s[1] == g and s[2] < c1 and s[3] > c0]
     if kind in ("iv", "is"):
-        return [("m", step[1])] + ([("q", step[1] - GROUPS)] if step[1] >= GROUPS else [])
+        g, h = step[1:]
+        return [s for s in plan if s[0] == "m" and s[1] == g and s[2] < (h + 1) * N and s[3] > h * N] + (
+            [("q", g - 2, h)] if g >= 2 else [])
     if kind == "q":
-        u = step[1]
-        return ([("iv", u)] if V_COLS[u] > 0 else []) + ([("is", u)] if V_COLS[u] < N else [])
+        return [s for s in plan if s[0] in ("iv", "is") and s[1:] == step[1:]]
     if kind == "mx":
         n, g = step[1:]
-        h, rt = divmod(n, RT)
-        out = [("q", h * GROUPS + g)] + [("gs", q) for q in range(4)]
-        rts = range(rt - rt % 4, rt - rt % 4 + 4) if n // 4 in C_CHUNKS else [rt]
-        out += [s for s in loads if s[0] == "G" and s[1] <= g < s[2] and any(s[3] <= x < s[4] for x in rts)]
+        rt, h = divmod(n, HALVES)
+        out = [("q", g, h)] + [s for s in plan if s[0] == "gs" and s[2] <= rt < s[3]]
+        out += [s for s in plan if s[0] == "G" and s[1] <= g < s[2] and s[3] <= rt < s[4]]
         if g > 0:
             out.append(("mx", n, g - 1))
-        elif n >= MX_BANKS:
-            out.append(scale_step(n - MX_BANKS))
+        elif n >= BANKS:
+            out.append(("z", [i for i in range(n) if sum_bank(i) == sum_bank(n)][-1]))
+        elif n == BANKS - 1:
+            out.append(("gb",))
         return out
     if kind == "z":
         return [("mx", step[1], GROUPS - 1), ("gb",)]
     if kind in ("y", "yg", "yb"):
-        n = step[1]
-        out = [("tc" if n // 4 in C_CHUNKS else "z", n)] + [s for s in loads if s[0] == "f" and s[1] <= n < s[2]]
+        rt, c0, c1 = step[1:]
+        out = [("z", rt * HALVES + h) for h in range(c0 // N, (c1 - 1) // N + 1)]
+        out += [s for s in plan if s[0] == "f" and s[1] <= rt < s[2]]
         if kind == "yb":
-            return out + [("t", turn_of(n - Y16_BUFS))]
-        return out + ([("yb", n)] if n in V_CAST else [])
-    if kind in ("c", "cg"):
-        n = step[1]
-        return [add_step(n)] + ([("t", turn_of(n - Y16_BUFS))] if n >= Y16_BUFS else [])
+            return out + [s for s in plan if s[0] == "t" and s[1] == rt - Y16_BUFS]
+        return out + [s for s in plan if s[0] == "yb" and s[1] == rt and s[2] < c1 and s[3] > c0]
+    if kind == "c":
+        rt, c0, c1 = step[1:]
+        out = [s for s in plan if s[0] in ("y", "yg") and s[1] == rt and s[2] < c1 and s[3] > c0]
+        return out + [s for s in plan if s[0] == "t" and s[1] == rt - Y16_BUFS]
     if kind == "t":
-        k = step[1]
-        return [cast_step(n) for n in range(*TURNS[k])] + [("ident",)] + t_bank_free(step)
+        rt, c0, c1 = step[1:]
+        turns = [s for s in TURNS]
+        i = turns.index(step[1:])
+        last = ("p",) + turns[i - 2] if i >= 2 else ("z", MX_BANKS + i)
+        return [s for s in plan if s[0] in ("c", "yb") and s[1] == rt and s[2] < c1 and s[3] > c0] + [("ident",), last]
     if kind == "p":
-        return [("t", step[1])] + ([("qy", step[1] - YT_BUFS)] if step[1] >= YT_BUFS else [])
+        rt = step[1]
+        old = rt - 2 * CHUNK
+        return [("t",) + step[1:]] + [s for s in plan if s[0] == "qy" and s[2] <= old < s[3]]
     if kind == "qy":
-        return [("p", step[1])]
+        h, r0, r1 = step[1:]
+        return [s for s in plan if s[0] == "p" and r0 <= s[1] < r1 and s[2] <= h * N < s[3]]
     if kind == "sy":
-        return [add_step(n) for n in range(step[1], step[2])]
-    if kind == "sw":
-        return [("qy", turn_of(n)) for n in range(step[1], step[2])]
-    if kind in ("ss", "ss2"):
-        return [("qy", turn_of(n)) for n in range(step[1] * RT, (step[1] + 1) * RT)]
+        r0, r1, c0, c1 = step[1:]
+        return [s for s in plan if s[0] in ("y", "yg") and r0 <= s[1] < r1 and s[2] < c1 and s[3] > c0]
+    if kind in ("sw", "ss", "ss2"):
+        r0, r1 = step[1:3]
+        return [s for s in plan if s[0] == "qy" and s[2] < r1 and s[3] > r0]
     return []
 
 
-def turn_of(n):
-    return [k for k, (n0, n1) in enumerate(TURNS) if n0 <= n < n1][0]
-
-
-def scale_step(n):
-    return ("zc" if n // 4 in C_CHUNKS else "z", n)
-
-
-def t_bank_free(step):
-    i = T_USES.index(step)
-    if i < T_BANKS:
-        return [("gb",)] + ([("cb",)] if C_CHUNKS else [])
-    kind, k = T_USES[i - T_BANKS]
-    return [("p", k) if kind == "t" else ("y", k)]
-
-
-def add_step(n):
-    return ("yg" if n in G_ADD else "y", n)
-
-
-def cast_step(n):
-    return ("cg" if n in G_CAST else "yb" if n in V_CAST else "c", n)
-
-
-V_COLS = [256,256,256,128,128,0,0,0]
-G_ADD = ()
-G_CAST = ()
-V_CAST = (23,)
-C_CHUNKS = []
-MX_BANKS = 6
-T_BANKS = 2
-ZT_BUFS = 1
-TURNS = [(n, n + 2) for n in range(0, 22, 2)] + [(22, 23), (23, 24)]
-T_USES = [("t", k) for k in range(len(TURNS))]
-LOADS = (
-    [("area",), ("d", 0), ("d", 1), ("gain",), ("d", 2), ("d", 3)] + [("gs", q) for q in range(4)]
-    + [("G", 0, 2, 0, 4), ("d", 4), ("G", 2, 4, 0, 4), ("d", 5), ("G", 0, 4, 4, 6), ("d", 6),
-       ("G", 0, 4, 6, 8), ("G", 0, 4, 8, 12), ("d", 7), ("f", 0, 4), ("f", 4, 8), ("f", 8, 12), ("f", 12, 18), ("f", 18, 24)]
-)
+V_COLS = [[256,256],[224,224],[224,224],[192,256]]
+G_COLS = 512
+TURNS = [(rt, 0, C) for rt in range(RT - 1)] + [(RT - 1, 0, N), (RT - 1, N, C)]
 
 
 def engine_orders():
-    sync = list(LOADS)
-    sync += [("sy", 0, 4), ("sy", 4, 8), ("sy", 8, 12), ("sw", 0, 6), ("sy", 12, 16), ("sw", 6, 12)] + [("ss", 0, q) for q in range(4)] + [("sy", 16, 18), ("sy", 18, 20), ("sw", 12, 16), ("sy", 20, 22), ("sy", 22, 23), ("sw", 16, 20), ("sy", 23, 24), ("sw", 20, 24), ("ss", 1, 0), ("ss", 1, 1)]
+    sync = [("area",), ("d", 0, 0, N), ("d", 0, N, C), ("d", 1, 0, C), ("d", 2, 0, C)] + [("gs", q, 0, 4) for q in range(4)] + [("gain",), ("G", 0, 2, 0, 4), ("d", 3, 0, N), ("G", 2, 4, 0, 2), ("d", 3, N, C), ("G", 2, 4, 2, 4)] + [("gs", q, 4, 12) for q in range(4)] + [("G", 0, 4, 4, 6), ("f", 0, 2), ("G", 0, 4, 6, 8), ("f", 2, 6), ("G", 0, 4, 8, 12), ("f", 6, 12)]
+    sync += [("sy", 0, 2, 0, C), ("sy", 2, 4, 0, C), ("sy", 4, 6, 0, C), ("sw", 0, 4), ("sy", 6, 8, 0, C), ("sy", 8, 10, 0, C), ("sw", 4, 8)] + [("ss", 0, 8, q) for q in range(4)] + [("sy", 10, 11, 0, C), ("sw", 8, 10), ("sy", 11, 12, 0, N), ("sy", 11, 12, N, C), ("sw", 10, 12), ("ss", 8, 12, 0), ("ss", 8, 12, 1)]
 
-    vec = [("init",), ("m", 0)]
-    for u in range(1, 6):
-        vec += [("iv", u - 1), ("m", u), ("q", u - 1)]
-    vec = [s for s in vec if s[0] != "iv" or V_COLS[s[1]]]
-    vec += [("z", 0), ("z", 1), ("z", 2), ("m", 6), ("z", 3), ("z", 4), ("q", 5), ("z", 5), ("z", 6), ("m", 7), ("q", 6), ("z", 7), ("y", 0), ("y", 1), ("z", 8), ("q", 7)]
-    zs = [n for n in range(TILES) if ("z", n) not in vec]
-    ys = [n for n in range(TILES - 1) if ("y", n) not in vec]
+    vec = [("init",), ("m", 0, 0, N), ("iv", 0, 0), ("m", 0, N, C), ("q", 0, 0), ("iv", 0, 1), ("m", 1, 0, C), ("q", 0, 1), ("iv", 1, 0), ("iv", 1, 1), ("m", 2, 0, C), ("q", 1, 0), ("iv", 2, 0), ("q", 1, 1), ("iv", 2, 1), ("m", 3, 0, N), ("q", 2, 0), ("iv", 3, 0), ("q", 2, 1), ("m", 3, N, C), ("q", 3, 0), ("iv", 3, 1), ("q", 3, 1), ("z", 0), ("z", 2)]
+    vec = [s for s in vec if s[0] != "iv" or V_COLS[s[1]][s[2]]]
+    gps = [("ident",)]
+    quant = {6: [("qy", 0, 0, 4), ("qy", 1, 0, 4)], 8: [("qy", 0, 4, 8), ("qy", 1, 4, 8)]}
+    for rt in range(0, RT - 2, 2):
+        vec += [("z", n) for n in range(2 * rt, 2 * rt + 4) if ("z", n) not in vec]
+        if G_COLS:
+            gps.append(("yg", rt, 0, G_COLS))
+        vec += [("y", rt + 1, 0, C), ("y", rt, G_COLS, C)] if False else [("y", rt, G_COLS, C), ("y", rt + 1, 0, C)]
+        vec += quant.get(rt, [])
+    vec += [("z", 20), ("z", 21), ("z", 22), ("z", 23), ("y", 10, G_COLS, C), ("y", 11, 0, N), ("yb", 11, N, C), ("qy", 0, 8, 10), ("qy", 1, 8, 10), ("y", 11, N, C), ("qy", 0, 10, 12), ("qy", 1, 10, 11), ("qy", 1, 11, 12)]
+    gps += [("yg", 10, 0, G_COLS)]
+
+    act = [("ones",)] + [("is", g, h) for g in range(GROUPS) for h in range(HALVES)]
+    act.insert(6, ("gb",))
+    act = [s for s in act if s[0] != "is" or V_COLS[s[1]][s[2]] < N]
+    for rt in range(0, RT - 2, 2):
+        act += [("p",) + turn for turn in TURNS[max(rt - 2, 0) : rt]] + [("c", rt, 0, C), ("c", rt + 1, 0, C)]
+    act += [("p", 8, 0, C), ("p", 9, 0, C), ("c", 10, 0, C), ("c", 11, 0, N), ("p", 10, 0, C), ("p", 11, 0, N), ("p", 11, N, C), ("ss2", 8, 12, 2), ("ss2", 8, 12, 3)]
+
+    pe = [("gmm",)] + [("mx", n, g) for g in (0, 1) for n in (0, 2, 1, 3)] + [("mx", n, g) for g in (0,) for n in (4, 6, 5, 7)] + [("mx", n, g) for g in (2,) for n in (0, 2, 1, 3)] + [("mx", n, g) for g in (1,) for n in (4, 6, 5, 7)] + [("mx", n, g) for g in (3,) for n in (0, 2, 1, 3)] + [("mx", n, g) for g in (2, 3) for n in (4, 6, 5, 7)]
     k = 0
-    while ys:
-        if zs:
-            vec.append(("z", zs.pop(0)))
-        for i in range(2 if len(ys) > len(zs) + 1 else 1):
-            n = ys.pop(0)
-            vec.append(("y", n))
-            if n % 2 == 1 and n >= 7:
-                vec.append(("qy", k))
-                k += 1
-    vec.insert(vec.index(("y", TILES - 2)), ("yb", TILES - 1))
-    vec.insert(vec.index(("y", TILES - 2)) + 1, ("y", TILES - 1))
-    vec += [("qy", j) for j in range(k, len(TURNS))]
-
-    act = [("ones",)] + [("is", u) for u in range(4)] + [("gb",)]
-    act += [("is", u) for u in range(4, 8)]
-    act = [s for s in act if s[0] != "is" or V_COLS[s[1]] < N]
-    for k in range(PAIRS - 1):
-        act += [("c", 2 * k), ("c", 2 * k + 1)] + ([("p", k - 1)] if k >= 1 else [])
-    act += [("c", 22)] + [("p", k) for k in range(PAIRS - 1 - 1, len(TURNS))] + [("ss2", 1, 2), ("ss2", 1, 3)]
-
-    pe = [("gmm",)] + [("mx", n, g) for g in range(GROUPS) for n in range(4)]
-    pe += [("mx", n, g) for n in range(4, 15) for g in range(GROUPS)]
-    k = 0
-    for n in range(15, TILES, 2):
-        pe += [("t", k), ("t", k + 1)] + [("mx", i, g) for i in range(n, min(n + 2, TILES)) for g in range(GROUPS)]
-        k += 2
-    pe += [("t", j) for j in range(k, len(TURNS))]
-    return [sync, vec, act, pe, [("ident",)]]
+    for n in range(BANKS, SUMS):
+        pe += [("mx", n, g) for g in range(GROUPS)]
+        if n in (11, 14, 17, 20):
+            pe += [("t",) + TURNS[k], ("t",) + TURNS[k + 1]]
+            k += 2
+    pe += [("t",) + turn for turn in TURNS[k:]]
+    return [sync, vec, act, pe, gps]
 
 
 def tile_winding_dipole_sum_k2_kernel(
@@ -193,25 +157,25 @@ def tile_winding_dipole_sum_k2_kernel(
         ident = sb.tile([P, P], F32)
         gw = sb.tile([P, GROUPS, R], U32, align_bytes=64)
         gs = sb.tile([P, GROUPS, R], U8, align_bytes=64)
-        rows = sb.tile([P, UNITS, PACK, N], BF16, align_bytes=64)
-        packed = sb.tile([P, GROUPS, N, PACK], BF16, align_bytes=64)
-        aw = sb.tile([P, UNITS, N], U32, align_bytes=64)
-        asc = sb.tile([P, UNITS, N], U8, align_bytes=64)
-        fld = sb.tile([P, TILES, N], BF16, align_bytes=64)
-        y = sb.tile([P, TILES, N], F32, align_bytes=64)
-        y16 = sb.tile([P, Y16_BUFS, N], BF16, align_bytes=64)
-        yt = sb.tile([P, YT_BUFS, 2 * P, PACK], BF16, align_bytes=64)
+        rows = sb.tile([P, GROUPS, PACK, C], BF16, align_bytes=64)
+        packed = sb.tile([P, 2, C, PACK], BF16, align_bytes=64)
+        aw = sb.tile([P, GROUPS, C], U32, align_bytes=64)
+        asc = sb.tile([P, GROUPS, C], U8, align_bytes=64)
+        fld = sb.tile([P, RT, C], BF16, align_bytes=64)
+        y = sb.tile([P, RT, C], F32, align_bytes=64)
+        y16 = sb.tile([P, Y16_BUFS, 2, C // PACK, 2], BF16, align_bytes=64)
+        yt = sb.tile([P, 2, HALVES, CHUNK * P, PACK], BF16, align_bytes=64)
         yw = sb.tile([P, HALVES, R], U32, align_bytes=64)
         ysc = sb.tile([P, HALVES, R], U8, align_bytes=64)
-        banks = [ps.tile([P, N], F32, name="bank%d" % i) for i in range(8)]
+        banks = [ps.tile([P, N], F32, name="bank%d" % i) for i in range(BANKS)]
 
         g_src = g_words.rearrange("g p n t -> p g (n t)")
         w_dst = out_1.rearrange("g p m t -> p g (m t)")
+        pairs = "r (p u e) -> r u p e"
 
-        def hbm_tiles(ap, n0, n1):
-            h, r0 = divmod(n0, RT)
-            part = ap[r0 * P : (r0 + n1 - n0) * P, h * N : (h + 1) * N]
-            return part.rearrange("(a p) c -> p a c", p=P)
+        def turn_bank(step):
+            width = (step[3] - step[2]) // 2
+            return banks[MX_BANKS + TURNS.index(step[1:]) % 2][:, :width]
 
         def run(step):
             kind = step[0]
@@ -230,20 +194,20 @@ def tile_winding_dipole_sum_k2_kernel(
             elif kind == "gmm":
                 for h in range(HALVES):
                     nc.tensor.matmul(
-                        out=banks[7][:].bitcast(BF16)[:, h * N : (h + 1) * N],
+                        out=banks[BANKS - 1][:].bitcast(BF16)[:, h * N : (h + 1) * N],
                         lhsT=ones[:], rhs=gain_row[:, h * N : (h + 1) * N], start=True, stop=True,
                     )
             elif kind == "gb":
-                nc.scalar.copy(out=gain_all[:], in_=banks[7][:].bitcast(BF16))
+                nc.scalar.copy(out=gain_all[:], in_=banks[BANKS - 1][:].bitcast(BF16))
             elif kind == "d":
-                h, g = divmod(step[1], GROUPS)
-                src = density[g * KP : (g + 1) * KP, h * N : (h + 1) * N]
-                nc.sync.dma_start(out=rows[:, step[1]], in_=src.rearrange("(p t) c -> p t c", t=PACK))
+                g, c0, c1 = step[1:]
+                src = density[g * KP : (g + 1) * KP, c0:c1]
+                nc.sync.dma_start(out=rows[:, g, :, c0:c1], in_=src.rearrange("(p t) c -> p t c", t=PACK))
             elif kind == "gs":
-                q = step[1]
+                q, r0, r1 = step[1:]
                 nc.sync.dma_start(
-                    out=gs[32 * q : 32 * q + 4].bitcast(I32),
-                    in_=g_scales[:, 4 * q : 4 * q + 4, :].rearrange("g j n -> j g n").bitcast(I32),
+                    out=gs[32 * q : 32 * q + 4, :, r0 * P : r1 * P].bitcast(I32),
+                    in_=g_scales[:, 4 * q : 4 * q + 4, r0 * P : r1 * P].rearrange("g j n -> j g n").bitcast(I32),
                 )
             elif kind == "G":
                 g0, g1, r0, r1 = step[1:]
@@ -252,108 +216,117 @@ def tile_winding_dipole_sum_k2_kernel(
                     in_=g_src[:, g0:g1, r0 * P * PACK : r1 * P * PACK].bitcast(I32),
                 )
             elif kind == "f":
-                nc.sync.dma_start(out=fld[:, step[1] : step[2]], in_=hbm_tiles(field, step[1], step[2]))
+                r0, r1 = step[1:]
+                nc.sync.dma_start(
+                    out=fld[:, r0:r1], in_=field[r0 * P : r1 * P, :].rearrange("(a p) c -> p a c", p=P)
+                )
             elif kind == "m":
-                u = step[1]
+                g, c0, c1 = step[1:]
                 for t in range(PACK):
                     nc.vector.tensor_scalar(
-                        out=rows[:, u, t], in0=rows[:, u, t], scalar1=area[:, u % GROUPS, t : t + 1],
+                        out=rows[:, g, t, c0:c1], in0=rows[:, g, t, c0:c1], scalar1=area[:, g, t : t + 1],
                         scalar2=None, op0=MULT,
                     )
             elif kind in ("iv", "is"):
-                u = step[1]
-                cols = slice(0, V_COLS[u]) if kind == "iv" else slice(V_COLS[u], N)
-                dst = packed[:, u % GROUPS, cols].rearrange("p (c i) t -> p c t i", i=4)
-                src = rows[:, u, :, cols].rearrange("p t (c i) -> p c t i", i=4)
+                g, h = step[1:]
+                cut = h * N + V_COLS[g][h]
+                cols = slice(h * N, cut) if kind == "iv" else slice(cut, (h + 1) * N)
+                dst = packed[:, g % 2, cols].rearrange("p (c i) t -> p c t i", i=4)
+                src = rows[:, g, :, cols].rearrange("p t (c i) -> p c t i", i=4)
                 if kind == "iv":
                     nc.vector.tensor_copy(out=dst, in_=src)
                 else:
                     nc.scalar.copy(out=dst, in_=src)
             elif kind == "q":
-                u = step[1]
+                g, h = step[1:]
+                cols = slice(h * N, (h + 1) * N)
                 nc.vector.quantize_mx(
-                    out=aw[:, u].bitcast(E4M3), scales=asc[:, u],
-                    in_=packed[:, u % GROUPS].rearrange("p c t -> p (c t)"),
+                    out=aw[:, g, cols].bitcast(E4M3), scales=asc[:, g, cols],
+                    in_=packed[:, g % 2, cols].rearrange("p c t -> p (c t)"),
                 )
             elif kind == "mx":
                 n, g = step[1:]
-                h, rt = divmod(n, RT)
-                cols = slice(rt * P, (rt + 1) * P)
+                rt, h = divmod(n, HALVES)
+                qs = slice(rt * P, (rt + 1) * P)
+                cols = slice(h * N, (h + 1) * N)
                 nc.tensor.matmul_mx(
-                    out=banks[n % MX_BANKS][:],
-                    lhsT=gw[:, g, cols].bitcast(E5M2), lhsT_scale=gs[:, g, cols],
-                    rhs=aw[:, h * GROUPS + g].bitcast(E4M3), rhs_scale=asc[:, h * GROUPS + g],
+                    out=banks[sum_bank(n)][:],
+                    lhsT=gw[:, g, qs].bitcast(E5M2), lhsT_scale=gs[:, g, qs],
+                    rhs=aw[:, g, cols].bitcast(E4M3), rhs_scale=asc[:, g, cols],
                     start=(g == 0), stop=(g == GROUPS - 1),
                 )
             elif kind == "z":
-                n = step[1]
-                h = n // RT
+                rt, h = divmod(step[1], HALVES)
+                cols = slice(h * N, (h + 1) * N)
                 nc.vector.tensor_tensor(
-                    out=y[:, n], in0=banks[n % MX_BANKS][:], in1=gain_all[:, h * N : (h + 1) * N], op=MULT
+                    out=y[:, rt, cols], in0=banks[sum_bank(step[1])][:], in1=gain_all[:, cols], op=MULT
                 )
             elif kind in ("y", "yg"):
-                n = step[1]
+                rt, c0, c1 = step[1:]
                 eng = nc.vector if kind == "y" else nc.gpsimd
-                eng.tensor_tensor(out=y[:, n], in0=y[:, n], in1=fld[:, n], op=ADD)
-            elif kind in ("c", "cg"):
-                n = step[1]
-                dst = y16[:, n % Y16_BUFS].rearrange("r (u p e) -> r u p e", u=2, e=2)
-                src = y[:, n].rearrange("r (p u e) -> r u p e", u=2, e=2)
-                if kind == "c":
-                    nc.scalar.copy(out=dst, in_=src)
-                else:
-                    nc.gpsimd.tensor_scalar(out=dst, in0=src, scalar1=1.0, scalar2=-0.0, op0=MULT, op1=ADD)
+                eng.tensor_tensor(out=y[:, rt, c0:c1], in0=y[:, rt, c0:c1], in1=fld[:, rt, c0:c1], op=ADD)
             elif kind == "yb":
-                n = step[1]
-                order = "r (p u e) -> r u p e"
+                rt, c0, c1 = step[1:]
                 nc.vector.tensor_tensor(
-                    out=y16[:, n % Y16_BUFS].rearrange("r (u p e) -> r u p e", u=2, e=2),
-                    in0=y[:, n].rearrange(order, u=2, e=2), in1=fld[:, n].rearrange(order, u=2, e=2), op=ADD,
+                    out=y16[:, rt % Y16_BUFS, :, c0 // PACK : c1 // PACK],
+                    in0=y[:, rt, c0:c1].rearrange(pairs, u=2, e=2),
+                    in1=fld[:, rt, c0:c1].rearrange(pairs, u=2, e=2), op=ADD,
+                )
+            elif kind == "c":
+                rt, c0, c1 = step[1:]
+                nc.scalar.copy(
+                    out=y16[:, rt % Y16_BUFS, :, c0 // PACK : c1 // PACK],
+                    in_=y[:, rt, c0:c1].rearrange(pairs, u=2, e=2),
                 )
             elif kind == "t":
-                n0, n1 = TURNS[step[1]]
-                w = (n1 - n0) * P
-                bank = banks[MX_BANKS + step[1] % T_BANKS][:, : 2 * w].rearrange("p (u r) -> p u r", u=2)
-                for j in range(n1 - n0):
-                    words = y16[:, (n0 + j) % Y16_BUFS].bitcast(F32)
+                rt, c0, c1 = step[1:]
+                bank = turn_bank(step).rearrange("p (h u r) -> p h u r", u=2, r=P)
+                words = y16[:, rt % Y16_BUFS].rearrange("r u p e -> r u (p e)").bitcast(F32)
+                for h in range(c0 // N, c1 // N):
                     for u in range(2):
-                        nc.tensor.transpose(bank[:, u, j * P : (j + 1) * P], words[:, u * P : (u + 1) * P], ident[:])
+                        nc.tensor.transpose(bank[:, h - c0 // N, u], words[:, u, h * P : (h + 1) * P], ident[:])
             elif kind == "p":
-                n0, n1 = TURNS[step[1]]
-                w = (n1 - n0) * P
-                bank = banks[MX_BANKS + step[1] % T_BANKS][:, : 2 * w].rearrange("p (u r) -> p r u", u=2)
-                dst = yt[:, step[1] % YT_BUFS, :w].rearrange("p r t -> p (r t)").bitcast(F32)
-                nc.scalar.copy(out=dst.rearrange("p (r u) -> p r u", u=2), in_=bank)
+                rt, c0, c1 = step[1:]
+                bank = turn_bank(step).rearrange("p (h u r) -> p h r u", u=2, r=P)
+                a = rt % CHUNK
+                dst = yt[:, (rt // CHUNK) % 2, c0 // N : c1 // N, a * P : (a + 1) * P]
+                dst = dst.rearrange("p h r t -> p h (r t)").bitcast(F32)
+                nc.scalar.copy(out=dst.rearrange("p h (r u) -> p h r u", u=2), in_=bank)
             elif kind == "qy":
-                n0, n1 = TURNS[step[1]]
-                h, rt = divmod(n0, RT)
-                cols = slice(rt * P, (rt + n1 - n0) * P)
+                h, r0, r1 = step[1:]
+                a = r0 % CHUNK
+                src = yt[:, (r0 // CHUNK) % 2, h, a * P : (a + r1 - r0) * P]
                 nc.vector.quantize_mx(
-                    out=yw[:, h, cols].bitcast(E4M3), scales=ysc[:, h, cols],
-                    in_=yt[:, step[1] % YT_BUFS, : (n1 - n0) * P].rearrange("p r t -> p (r t)"),
+                    out=yw[:, h, r0 * P : r1 * P].bitcast(E4M3), scales=ysc[:, h, r0 * P : r1 * P],
+                    in_=src.rearrange("p r t -> p (r t)"),
                 )
             elif kind == "sy":
-                nc.sync.dma_start(out=hbm_tiles(out_0, step[1], step[2]), in_=y[:, step[1] : step[2]])
-            elif kind == "sw":
-                h, rt = divmod(step[1], RT)
-                r0, r1 = rt * P, (rt + step[2] - step[1]) * P
+                r0, r1, c0, c1 = step[1:]
                 nc.sync.dma_start(
-                    out=w_dst[:, h, r0 * PACK : r1 * PACK].bitcast(I32), in_=yw[:, h, r0:r1].bitcast(I32)
+                    out=out_0[r0 * P : r1 * P, c0:c1].rearrange("(a p) c -> p a c", p=P), in_=y[:, r0:r1, c0:c1]
+                )
+            elif kind == "sw":
+                r0, r1 = step[1:]
+                nc.sync.dma_start(
+                    out=w_dst[:, :, r0 * P * PACK : r1 * P * PACK].bitcast(I32),
+                    in_=yw[:, :, r0 * P : r1 * P].bitcast(I32),
                 )
             elif kind in ("ss", "ss2"):
-                h, q = step[1:]
+                r0, r1, q = step[1:]
                 eng = nc.sync if kind == "ss" else nc.scalar
                 eng.dma_start(
-                    out=out_2[h, 4 * q : 4 * q + 4, :].bitcast(I32), in_=ysc[32 * q : 32 * q + 4, h].bitcast(I32)
+                    out=out_2[:, 4 * q : 4 * q + 4, r0 * P : r1 * P].rearrange("g j m -> j g m").bitcast(I32),
+                    in_=ysc[32 * q : 32 * q + 4, :, r0 * P : r1 * P].bitcast(I32),
                 )
 
         queues = engine_orders()
+        plan = [s for queue in queues for s in queue]
         done = set()
         with tc.manual_schedule():
             while any(queues):
                 moved = False
                 for queue in queues:
-                    while queue and all(need in done for need in needs(queue[0], LOADS)):
+                    while queue and all(need in done for need in needs(queue[0], plan)):
                         step = queue.pop(0)
                         run(step)
                         done.add(step)

@@ -15,130 +15,25 @@ ADD = mybir.AluOpType.add
 
 R, K, C = 1536, 2048, 1024
 FLOPS = 2 * R * K * C
+
 P = 128
 PACK = 4
-KP = P * PACK
 N = 512
-GROUPS = K // KP
+GROUPS = K // (P * PACK)
 HALVES = C // N
-RT = R // P
-SUMS = RT * HALVES
+TILES = R // P
+QUADRANTS = 4
+
 BANKS = 8
-MX_BANKS = 6
-Y16_BUFS = 6
+FIRST_SUMS = [(tile, half) for half in range(HALVES) for tile in range(BANKS)]
+SUMS = FIRST_SUMS + [(tile, half) for tile in range(BANKS, TILES) for half in range(HALVES)]
+SUM_BANKS = 6
+TURNS = [(tile, 0, C) for tile in range(TILES - 1)] + [(TILES - 1, 0, N), (TILES - 1, N, C)]
+ROUNDED_BUFS = 6
 CHUNK = 4
 
-
-def sum_bank(n):
-    return n if n < BANKS else (n - BANKS) % MX_BANKS
-
-
-def covering(steps, kind, rt, h):
-    return [s for s in steps if s[0] in kind and s[1] == rt and s[2] < (h + 1) * N and s[3] > h * N]
-
-
-def needs(step, plan):
-    kind = step[0]
-    if kind in ("gs", "ones", "gain"):
-        return [("init",)]
-    if kind == "gmm":
-        return [("ones",), ("gain",)]
-    if kind == "gb":
-        return [("gmm",)]
-    if kind == "m":
-        g, c0, c1 = step[1:]
-        return [("area",)] + [s for s in plan if s[0] == "d" and s[1] == g and s[2] < c1 and s[3] > c0]
-    if kind in ("iv", "is"):
-        g, h = step[1:]
-        return [s for s in plan if s[0] == "m" and s[1] == g and s[2] < (h + 1) * N and s[3] > h * N] + (
-            [("q", g - 2, h)] if g >= 2 else [])
-    if kind == "q":
-        return [s for s in plan if s[0] in ("iv", "is") and s[1:] == step[1:]]
-    if kind == "mx":
-        n, g = step[1:]
-        rt, h = divmod(n, HALVES)
-        out = [("q", g, h)] + [s for s in plan if s[0] == "gs" and s[2] <= rt < s[3]]
-        out += [s for s in plan if s[0] == "G" and s[1] <= g < s[2] and s[3] <= rt < s[4]]
-        if g > 0:
-            out.append(("mx", n, g - 1))
-        elif n >= BANKS:
-            out.append(("z", [i for i in range(n) if sum_bank(i) == sum_bank(n)][-1]))
-        elif n == BANKS - 1:
-            out.append(("gb",))
-        return out
-    if kind == "z":
-        return [("mx", step[1], GROUPS - 1), ("gb",)]
-    if kind in ("y", "yg", "yb"):
-        rt, c0, c1 = step[1:]
-        out = [("z", rt * HALVES + h) for h in range(c0 // N, (c1 - 1) // N + 1)]
-        out += [s for s in plan if s[0] == "f" and s[1] <= rt < s[2]]
-        if kind == "yb":
-            return out + [s for s in plan if s[0] == "t" and s[1] == rt - Y16_BUFS]
-        return out + [s for s in plan if s[0] == "yb" and s[1] == rt and s[2] < c1 and s[3] > c0]
-    if kind == "c":
-        rt, c0, c1 = step[1:]
-        out = [s for s in plan if s[0] in ("y", "yg") and s[1] == rt and s[2] < c1 and s[3] > c0]
-        return out + [s for s in plan if s[0] == "t" and s[1] == rt - Y16_BUFS]
-    if kind == "t":
-        rt, c0, c1 = step[1:]
-        turns = [s for s in TURNS]
-        i = turns.index(step[1:])
-        last = ("p",) + turns[i - 2] if i >= 2 else ("z", MX_BANKS + i)
-        return [s for s in plan if s[0] in ("c", "yb") and s[1] == rt and s[2] < c1 and s[3] > c0] + [("ident",), last]
-    if kind == "p":
-        rt = step[1]
-        old = rt - 2 * CHUNK
-        return [("t",) + step[1:]] + [s for s in plan if s[0] == "qy" and s[2] <= old < s[3]]
-    if kind == "qy":
-        h, r0, r1 = step[1:]
-        return [s for s in plan if s[0] == "p" and r0 <= s[1] < r1 and s[2] <= h * N < s[3]]
-    if kind == "sy":
-        r0, r1, c0, c1 = step[1:]
-        return [s for s in plan if s[0] in ("y", "yg") and r0 <= s[1] < r1 and s[2] < c1 and s[3] > c0]
-    if kind in ("sw", "ss", "ss2"):
-        r0, r1 = step[1:3]
-        return [s for s in plan if s[0] == "qy" and s[2] < r1 and s[3] > r0]
-    return []
-
-
-V_COLS = [[256,256],[224,224],[224,224],[192,256]]
-G_COLS = 512
-TURNS = [(rt, 0, C) for rt in range(RT - 1)] + [(RT - 1, 0, N), (RT - 1, N, C)]
-
-
-def engine_orders():
-    sync = [("area",), ("d", 0, 0, N), ("d", 0, N, C), ("d", 1, 0, C), ("d", 2, 0, C)] + [("gs", q, 0, 4) for q in range(4)] + [("gain",), ("G", 0, 2, 0, 4), ("d", 3, 0, N), ("G", 2, 4, 0, 2), ("d", 3, N, C), ("G", 2, 4, 2, 4)] + [("gs", q, 4, 12) for q in range(4)] + [("G", 0, 4, 4, 6), ("f", 0, 2), ("G", 0, 4, 6, 8), ("f", 2, 6), ("G", 0, 4, 8, 12), ("f", 6, 12)]
-    sync += [("sy", 0, 2, 0, C), ("sy", 2, 4, 0, C), ("sy", 4, 6, 0, C), ("sw", 0, 4), ("sy", 6, 8, 0, C), ("sy", 8, 10, 0, C), ("sw", 4, 8)] + [("ss", 0, 8, q) for q in range(4)] + [("sy", 10, 11, 0, C), ("sw", 8, 10), ("sy", 11, 12, 0, N), ("sy", 11, 12, N, C), ("sw", 10, 12), ("ss", 8, 12, 0), ("ss", 8, 12, 1)]
-
-    vec = [("init",), ("m", 0, 0, N), ("iv", 0, 0), ("m", 0, N, C), ("q", 0, 0), ("iv", 0, 1), ("m", 1, 0, C), ("q", 0, 1), ("iv", 1, 0), ("iv", 1, 1), ("m", 2, 0, C), ("q", 1, 0), ("iv", 2, 0), ("q", 1, 1), ("iv", 2, 1), ("m", 3, 0, N), ("q", 2, 0), ("iv", 3, 0), ("q", 2, 1), ("m", 3, N, C), ("q", 3, 0), ("iv", 3, 1), ("q", 3, 1), ("z", 0), ("z", 2)]
-    vec = [s for s in vec if s[0] != "iv" or V_COLS[s[1]][s[2]]]
-    gps = [("ident",)]
-    quant = {6: [("qy", 0, 0, 4), ("qy", 1, 0, 4)], 8: [("qy", 0, 4, 8), ("qy", 1, 4, 8)]}
-    for rt in range(0, RT - 2, 2):
-        vec += [("z", n) for n in range(2 * rt, 2 * rt + 4) if ("z", n) not in vec]
-        if G_COLS:
-            gps.append(("yg", rt, 0, G_COLS))
-        vec += [("y", rt + 1, 0, C), ("y", rt, G_COLS, C)] if False else [("y", rt, G_COLS, C), ("y", rt + 1, 0, C)]
-        vec += quant.get(rt, [])
-    vec += [("z", 20), ("z", 21), ("z", 22), ("z", 23), ("y", 10, G_COLS, C), ("y", 11, 0, N), ("yb", 11, N, C), ("qy", 0, 8, 10), ("qy", 1, 8, 10), ("y", 11, N, C), ("qy", 0, 10, 12), ("qy", 1, 10, 11), ("qy", 1, 11, 12)]
-    gps += [("yg", 10, 0, G_COLS)]
-
-    act = [("ones",)] + [("is", g, h) for g in range(GROUPS) for h in range(HALVES)]
-    act.insert(6, ("gb",))
-    act = [s for s in act if s[0] != "is" or V_COLS[s[1]][s[2]] < N]
-    for rt in range(0, RT - 2, 2):
-        act += [("p",) + turn for turn in TURNS[max(rt - 2, 0) : rt]] + [("c", rt, 0, C), ("c", rt + 1, 0, C)]
-    act += [("p", 8, 0, C), ("p", 9, 0, C), ("c", 10, 0, C), ("c", 11, 0, N), ("p", 10, 0, C), ("p", 11, 0, N), ("p", 11, N, C), ("ss2", 8, 12, 2), ("ss2", 8, 12, 3)]
-
-    pe = [("gmm",)] + [("mx", n, g) for g in (0, 1) for n in (0, 2, 1, 3)] + [("mx", n, g) for g in (0,) for n in (4, 6, 5, 7)] + [("mx", n, g) for g in (2,) for n in (0, 2, 1, 3)] + [("mx", n, g) for g in (1,) for n in (4, 6, 5, 7)] + [("mx", n, g) for g in (3,) for n in (0, 2, 1, 3)] + [("mx", n, g) for g in (2, 3) for n in (4, 6, 5, 7)]
-    k = 0
-    for n in range(BANKS, SUMS):
-        pe += [("mx", n, g) for g in range(GROUPS)]
-        if n in (11, 14, 17, 20):
-            pe += [("t",) + TURNS[k], ("t",) + TURNS[k + 1]]
-            k += 2
-    pe += [("t",) + turn for turn in TURNS[k:]]
-    return [sync, vec, act, pe, gps]
+VECTOR_COLS = (256, 160)
+GPSIMD_FROM = 384
 
 
 def tile_winding_dipole_sum_k2_kernel(
@@ -146,189 +41,325 @@ def tile_winding_dipole_sum_k2_kernel(
 ):
     nc = tc.nc
     with ExitStack() as ctx:
-        sb = ctx.enter_context(tc.tile_pool(name="sb", bufs=1))
-        ps = ctx.enter_context(tc.psum_pool(name="ps", bufs=1))
+        sbuf = ctx.enter_context(tc.tile_pool(name="sbuf", bufs=1))
+        psum = ctx.enter_context(tc.psum_pool(name="psum", bufs=1))
+        ctx.enter_context(tc.manual_schedule())
 
-        area = sb.tile([P, GROUPS, PACK], BF16)
-        gain_row = sb.tile([P, C], BF16)
-        gain_all = sb.tile([P, C], BF16)
-        ones_f32 = sb.tile([P, P], F32)
-        ones = sb.tile([P, P], BF16)
-        ident = sb.tile([P, P], F32)
-        gw = sb.tile([P, GROUPS, R], U32, align_bytes=64)
-        gs = sb.tile([P, GROUPS, R], U8, align_bytes=64)
-        rows = sb.tile([P, GROUPS, PACK, C], BF16, align_bytes=64)
-        packed = sb.tile([P, 2, C, PACK], BF16, align_bytes=64)
-        aw = sb.tile([P, GROUPS, C], U32, align_bytes=64)
-        asc = sb.tile([P, GROUPS, C], U8, align_bytes=64)
-        fld = sb.tile([P, RT, C], BF16, align_bytes=64)
-        y = sb.tile([P, RT, C], F32, align_bytes=64)
-        y16 = sb.tile([P, Y16_BUFS, 2, C // PACK, 2], BF16, align_bytes=64)
-        yt = sb.tile([P, 2, HALVES, CHUNK * P, PACK], BF16, align_bytes=64)
-        yw = sb.tile([P, HALVES, R], U32, align_bytes=64)
-        ysc = sb.tile([P, HALVES, R], U8, align_bytes=64)
-        banks = [ps.tile([P, N], F32, name="bank%d" % i) for i in range(BANKS)]
+        area = sbuf.tile([P, GROUPS, 16], BF16)
+        gain_row = sbuf.tile([P, C], BF16)
+        gain_all = sbuf.tile([P, C], BF16)
+        ones_f32 = sbuf.tile([P, P], F32)
+        ones = sbuf.tile([P, P], BF16)
+        ident = sbuf.tile([P, P], F32)
+        g_codes = sbuf.tile([P, GROUPS, R], U32, align_bytes=64)
+        g_bytes = sbuf.tile([P, GROUPS, R], U8, align_bytes=64)
+        rows = sbuf.tile([P, GROUPS, PACK, C], BF16, align_bytes=64)
+        packed = sbuf.tile([P, 2, C, PACK], BF16, align_bytes=64)
+        a_codes = sbuf.tile([P, GROUPS, C], U32, align_bytes=64)
+        a_bytes = sbuf.tile([P, GROUPS, C], U8, align_bytes=64)
+        field_sb = sbuf.tile([P, TILES, C], BF16, align_bytes=64)
+        y = sbuf.tile([P, TILES, C], F32, align_bytes=64)
+        rounded = sbuf.tile([P, ROUNDED_BUFS, 2, C // PACK, 2], BF16, align_bytes=64)
+        turned = sbuf.tile([P, 2, HALVES, CHUNK * P, PACK], BF16, align_bytes=64)
+        y_codes = sbuf.tile([P, HALVES, R], U32, align_bytes=64)
+        y_bytes = sbuf.tile([P, HALVES, R], U8, align_bytes=64)
+        banks = [psum.tile([P, N], F32, name="bank%d" % i) for i in range(BANKS)]
+        gain_bank = banks[BANKS - 1][:].bitcast(BF16)
 
-        g_src = g_words.rearrange("g p n t -> p g (n t)")
-        w_dst = out_1.rearrange("g p m t -> p g (m t)")
-        pairs = "r (p u e) -> r u p e"
+        def cols(half):
+            return slice(half * N, (half + 1) * N)
 
-        def turn_bank(step):
-            width = (step[3] - step[2]) // 2
-            return banks[MX_BANKS + TURNS.index(step[1:]) % 2][:, :width]
+        def span(first, end, width=P):
+            return slice(first * width, end * width)
 
-        def run(step):
-            kind = step[0]
-            if kind == "init":
-                nc.vector.memset(ones_f32[:], 1.0)
-                nc.vector.memset(gain_row[:], 0.0)
-                nc.vector.memset(gs[:].rearrange("p g n -> p (g n)").bitcast(U32), 0)
-            elif kind == "ident":
-                make_identity(nc, ident[:])
-            elif kind == "area":
-                nc.sync.dma_start(out=area[:], in_=area_weight.rearrange("(g p t) -> p g t", p=P, t=PACK))
-            elif kind == "ones":
-                nc.scalar.copy(out=ones[:], in_=ones_f32[:])
-            elif kind == "gain":
-                nc.sync.dma_start(out=gain_row[0:1, :], in_=gain.rearrange("(o c) -> o c", o=1))
-            elif kind == "gmm":
-                for h in range(HALVES):
-                    nc.tensor.matmul(
-                        out=banks[BANKS - 1][:].bitcast(BF16)[:, h * N : (h + 1) * N],
-                        lhsT=ones[:], rhs=gain_row[:, h * N : (h + 1) * N], start=True, stop=True,
-                    )
-            elif kind == "gb":
-                nc.scalar.copy(out=gain_all[:], in_=banks[BANKS - 1][:].bitcast(BF16))
-            elif kind == "d":
-                g, c0, c1 = step[1:]
-                src = density[g * KP : (g + 1) * KP, c0:c1]
-                nc.sync.dma_start(out=rows[:, g, :, c0:c1], in_=src.rearrange("(p t) c -> p t c", t=PACK))
-            elif kind == "gs":
-                q, r0, r1 = step[1:]
+        def sum_bank(n):
+            return banks[n if n < BANKS else (n - BANKS) % SUM_BANKS][:]
+
+        def turn_bank(i):
+            return banks[SUM_BANKS + i % 2][:, : (TURNS[i][2] - TURNS[i][1]) // 2]
+
+        def load_density(g, half):
+            src = density[span(g, g + 1, P * PACK), cols(half)]
+            nc.sync.dma_start(out=rows[:, g, :, cols(half)], in_=src.rearrange("(p t) c -> p t c", t=PACK))
+
+        def load_g_codes(g0, g1, tile0, tile1):
+            src = g_words.rearrange("g p r t -> p g (r t)")[:, g0:g1, span(tile0, tile1, P * PACK)]
+            nc.sync.dma_start(out=g_codes[:, g0:g1, span(tile0, tile1)].bitcast(I32), in_=src.bitcast(I32))
+
+        def load_g_bytes(tile0, tile1):
+            for q in range(QUADRANTS):
+                src = g_scales[:, 4 * q : 4 * q + 4, span(tile0, tile1)].rearrange("g j r -> j g r")
                 nc.sync.dma_start(
-                    out=gs[32 * q : 32 * q + 4, :, r0 * P : r1 * P].bitcast(I32),
-                    in_=g_scales[:, 4 * q : 4 * q + 4, r0 * P : r1 * P].rearrange("g j n -> j g n").bitcast(I32),
+                    out=g_bytes[32 * q : 32 * q + 4, :, span(tile0, tile1)].bitcast(I32), in_=src.bitcast(I32)
                 )
-            elif kind == "G":
-                g0, g1, r0, r1 = step[1:]
-                nc.sync.dma_start(
-                    out=gw[:, g0:g1, r0 * P : r1 * P].bitcast(I32),
-                    in_=g_src[:, g0:g1, r0 * P * PACK : r1 * P * PACK].bitcast(I32),
-                )
-            elif kind == "f":
-                r0, r1 = step[1:]
-                nc.sync.dma_start(
-                    out=fld[:, r0:r1], in_=field[r0 * P : r1 * P, :].rearrange("(a p) c -> p a c", p=P)
-                )
-            elif kind == "m":
-                g, c0, c1 = step[1:]
-                for t in range(PACK):
-                    nc.vector.tensor_scalar(
-                        out=rows[:, g, t, c0:c1], in0=rows[:, g, t, c0:c1], scalar1=area[:, g, t : t + 1],
-                        scalar2=None, op0=MULT,
-                    )
-            elif kind in ("iv", "is"):
-                g, h = step[1:]
-                cut = h * N + V_COLS[g][h]
-                cols = slice(h * N, cut) if kind == "iv" else slice(cut, (h + 1) * N)
-                dst = packed[:, g % 2, cols].rearrange("p (c i) t -> p c t i", i=4)
-                src = rows[:, g, :, cols].rearrange("p t (c i) -> p c t i", i=4)
-                if kind == "iv":
-                    nc.vector.tensor_copy(out=dst, in_=src)
-                else:
-                    nc.scalar.copy(out=dst, in_=src)
-            elif kind == "q":
-                g, h = step[1:]
-                cols = slice(h * N, (h + 1) * N)
-                nc.vector.quantize_mx(
-                    out=aw[:, g, cols].bitcast(E4M3), scales=asc[:, g, cols],
-                    in_=packed[:, g % 2, cols].rearrange("p c t -> p (c t)"),
-                )
-            elif kind == "mx":
-                n, g = step[1:]
-                rt, h = divmod(n, HALVES)
-                qs = slice(rt * P, (rt + 1) * P)
-                cols = slice(h * N, (h + 1) * N)
-                nc.tensor.matmul_mx(
-                    out=banks[sum_bank(n)][:],
-                    lhsT=gw[:, g, qs].bitcast(E5M2), lhsT_scale=gs[:, g, qs],
-                    rhs=aw[:, g, cols].bitcast(E4M3), rhs_scale=asc[:, g, cols],
-                    start=(g == 0), stop=(g == GROUPS - 1),
-                )
-            elif kind == "z":
-                rt, h = divmod(step[1], HALVES)
-                cols = slice(h * N, (h + 1) * N)
+
+        def load_field(tile0, tile1):
+            src = field[span(tile0, tile1), :].rearrange("(a p) c -> p a c", p=P)
+            nc.sync.dma_start(out=field_sb[:, tile0:tile1], in_=src)
+
+        def weigh(g, half):
+            for t in range(PACK):
+                row = rows[:, g, t, cols(half)]
+                nc.vector.tensor_scalar(out=row, in0=row, scalar1=area[:, g, t : t + 1], scalar2=None, op0=MULT)
+
+        def pack_views(g, c0, c1):
+            dst = packed[:, g % 2, c0:c1].rearrange("p (c i) t -> p c t i", i=4)
+            src = rows[:, g, :, c0:c1].rearrange("p t (c i) -> p c t i", i=4)
+            return dst, src
+
+        def pack_vector(g, half):
+            dst, src = pack_views(g, half * N, half * N + VECTOR_COLS[half])
+            nc.vector.tensor_copy(out=dst, in_=src)
+
+        def pack_scalar(g, half):
+            dst, src = pack_views(g, half * N + VECTOR_COLS[half], (half + 1) * N)
+            nc.scalar.copy(out=dst, in_=src)
+
+        def quantise_a(g, half):
+            nc.vector.quantize_mx(
+                out=a_codes[:, g, cols(half)].bitcast(E4M3),
+                scales=a_bytes[:, g, cols(half)],
+                in_=packed[:, g % 2, cols(half)].rearrange("p c t -> p (c t)"),
+            )
+
+        def mx_pass(n, g):
+            tile, half = SUMS[n]
+            nc.tensor.matmul_mx(
+                out=sum_bank(n),
+                lhsT=g_codes[:, g, span(tile, tile + 1)].bitcast(E5M2),
+                lhsT_scale=g_bytes[:, g, span(tile, tile + 1)],
+                rhs=a_codes[:, g, cols(half)].bitcast(E4M3),
+                rhs_scale=a_bytes[:, g, cols(half)],
+                start=(g == 0),
+                stop=(g == GROUPS - 1),
+            )
+
+        def by_group(sums, groups):
+            for g in groups:
+                for n in sums:
+                    mx_pass(n, g)
+
+        def by_sum(sums, groups=range(GROUPS)):
+            for n in sums:
+                for g in groups:
+                    mx_pass(n, g)
+
+        def apply_gain(*sums):
+            for n in sums:
+                tile, half = SUMS[n]
                 nc.vector.tensor_tensor(
-                    out=y[:, rt, cols], in0=banks[sum_bank(step[1])][:], in1=gain_all[:, cols], op=MULT
+                    out=y[:, tile, cols(half)], in0=sum_bank(n), in1=gain_all[:, cols(half)], op=MULT
                 )
-            elif kind in ("y", "yg"):
-                rt, c0, c1 = step[1:]
-                eng = nc.vector if kind == "y" else nc.gpsimd
-                eng.tensor_tensor(out=y[:, rt, c0:c1], in0=y[:, rt, c0:c1], in1=fld[:, rt, c0:c1], op=ADD)
-            elif kind == "yb":
-                rt, c0, c1 = step[1:]
-                nc.vector.tensor_tensor(
-                    out=y16[:, rt % Y16_BUFS, :, c0 // PACK : c1 // PACK],
-                    in0=y[:, rt, c0:c1].rearrange(pairs, u=2, e=2),
-                    in1=fld[:, rt, c0:c1].rearrange(pairs, u=2, e=2), op=ADD,
-                )
-            elif kind == "c":
-                rt, c0, c1 = step[1:]
-                nc.scalar.copy(
-                    out=y16[:, rt % Y16_BUFS, :, c0 // PACK : c1 // PACK],
-                    in_=y[:, rt, c0:c1].rearrange(pairs, u=2, e=2),
-                )
-            elif kind == "t":
-                rt, c0, c1 = step[1:]
-                bank = turn_bank(step).rearrange("p (h u r) -> p h u r", u=2, r=P)
-                words = y16[:, rt % Y16_BUFS].rearrange("r u p e -> r u (p e)").bitcast(F32)
-                for h in range(c0 // N, c1 // N):
+
+        def add_field(engine, tile, c0=0, c1=C):
+            part = y[:, tile, c0:c1]
+            engine.tensor_tensor(out=part, in0=part, in1=field_sb[:, tile, c0:c1], op=ADD)
+
+        def by_pairs(ap):
+            return ap.rearrange("r (w u e) -> r u w e", u=2, e=2)
+
+        def round_y(tile, c0=0, c1=C):
+            dst = rounded[:, tile % ROUNDED_BUFS, :, c0 // PACK : c1 // PACK]
+            nc.scalar.copy(out=dst, in_=by_pairs(y[:, tile, c0:c1]))
+
+        def turn(*turns):
+            for i in turns:
+                tile, c0, c1 = TURNS[i]
+                bank = turn_bank(i).rearrange("p (h u r) -> p h u r", u=2, r=P)
+                words = rounded[:, tile % ROUNDED_BUFS].rearrange("r u w e -> r u (w e)").bitcast(F32)
+                for half in range(c0 // N, c1 // N):
                     for u in range(2):
-                        nc.tensor.transpose(bank[:, h - c0 // N, u], words[:, u, h * P : (h + 1) * P], ident[:])
-            elif kind == "p":
-                rt, c0, c1 = step[1:]
-                bank = turn_bank(step).rearrange("p (h u r) -> p h r u", u=2, r=P)
-                a = rt % CHUNK
-                dst = yt[:, (rt // CHUNK) % 2, c0 // N : c1 // N, a * P : (a + 1) * P]
-                dst = dst.rearrange("p h r t -> p h (r t)").bitcast(F32)
-                nc.scalar.copy(out=dst.rearrange("p h (r u) -> p h r u", u=2), in_=bank)
-            elif kind == "qy":
-                h, r0, r1 = step[1:]
-                a = r0 % CHUNK
-                src = yt[:, (r0 // CHUNK) % 2, h, a * P : (a + r1 - r0) * P]
-                nc.vector.quantize_mx(
-                    out=yw[:, h, r0 * P : r1 * P].bitcast(E4M3), scales=ysc[:, h, r0 * P : r1 * P],
-                    in_=src.rearrange("p r t -> p (r t)"),
-                )
-            elif kind == "sy":
-                r0, r1, c0, c1 = step[1:]
-                nc.sync.dma_start(
-                    out=out_0[r0 * P : r1 * P, c0:c1].rearrange("(a p) c -> p a c", p=P), in_=y[:, r0:r1, c0:c1]
-                )
-            elif kind == "sw":
-                r0, r1 = step[1:]
-                nc.sync.dma_start(
-                    out=w_dst[:, :, r0 * P * PACK : r1 * P * PACK].bitcast(I32),
-                    in_=yw[:, :, r0 * P : r1 * P].bitcast(I32),
-                )
-            elif kind in ("ss", "ss2"):
-                r0, r1, q = step[1:]
-                eng = nc.sync if kind == "ss" else nc.scalar
-                eng.dma_start(
-                    out=out_2[:, 4 * q : 4 * q + 4, r0 * P : r1 * P].rearrange("g j m -> j g m").bitcast(I32),
-                    in_=ysc[32 * q : 32 * q + 4, :, r0 * P : r1 * P].bitcast(I32),
+                        nc.tensor.transpose(bank[:, half - c0 // N, u], words[:, u, span(half, half + 1)], ident[:])
+
+        def unload(*turns):
+            for i in turns:
+                tile, c0, c1 = TURNS[i]
+                place = span(tile % CHUNK, tile % CHUNK + 1)
+                dst = turned[:, (tile // CHUNK) % 2, c0 // N : c1 // N, place]
+                dst = dst.rearrange("p h r t -> p h (r t)").bitcast(F32).rearrange("p h (r u) -> p h r u", u=2)
+                nc.scalar.copy(out=dst, in_=turn_bank(i).rearrange("p (h u r) -> p h r u", u=2, r=P))
+
+        def quantise_y(half, tile0, tile1):
+            place = span(tile0 % CHUNK, tile0 % CHUNK + tile1 - tile0)
+            nc.vector.quantize_mx(
+                out=y_codes[:, half, span(tile0, tile1)].bitcast(E4M3),
+                scales=y_bytes[:, half, span(tile0, tile1)],
+                in_=turned[:, (tile0 // CHUNK) % 2, half, place].rearrange("p r t -> p (r t)"),
+            )
+
+        def store_y(tile0, tile1, c0=0, c1=C):
+            dst = out_0[span(tile0, tile1), c0:c1].rearrange("(a p) c -> p a c", p=P)
+            nc.sync.dma_start(out=dst, in_=y[:, tile0:tile1, c0:c1])
+
+        def store_codes(tile0, tile1):
+            dst = out_1.rearrange("h p r t -> p h (r t)")[:, :, span(tile0, tile1, P * PACK)]
+            nc.sync.dma_start(out=dst.bitcast(I32), in_=y_codes[:, :, span(tile0, tile1)].bitcast(I32))
+
+        def store_bytes(engine, quadrants, tile0, tile1):
+            for q in quadrants:
+                dst = out_2[:, 4 * q : 4 * q + 4, span(tile0, tile1)].rearrange("h j r -> j h r")
+                engine.dma_start(
+                    out=dst.bitcast(I32), in_=y_bytes[32 * q : 32 * q + 4, :, span(tile0, tile1)].bitcast(I32)
                 )
 
-        queues = engine_orders()
-        plan = [s for queue in queues for s in queue]
-        done = set()
-        with tc.manual_schedule():
-            while any(queues):
-                moved = False
-                for queue in queues:
-                    while queue and all(need in done for need in needs(queue[0], plan)):
-                        step = queue.pop(0)
-                        run(step)
-                        done.add(step)
-                        moved = True
-                assert moved
+
+        nc.vector.memset(ones_f32[:], 1.0)
+        nc.vector.memset(gain_row[:], 0.0)
+        nc.vector.memset(g_bytes[:].rearrange("p g r -> p (g r)").bitcast(U32), 0)
+        make_identity(nc, ident[:])
+        area_src = area_weight.rearrange("(g p t) -> p g t", p=P, t=PACK)
+        nc.scalar.dma_start(out=area[:, :1, :PACK], in_=area_src[:, :1])
+        nc.scalar.dma_start(out=area[:, 1:, :PACK], in_=area_src[:, 1:])
+        nc.scalar.copy(out=ones[:], in_=ones_f32[:])
+
+        load_density(0, 0)
+        load_density(1, 0)
+        load_g_bytes(0, 4)
+        load_density(2, 0)
+        nc.sync.dma_start(out=gain_row[0:1, :], in_=gain.rearrange("(o c) -> o c", o=1))
+        load_density(3, 0)
+        load_g_codes(0, 2, 0, 4)
+        load_g_codes(2, 4, 0, 4)
+        load_density(0, 1)
+        load_g_bytes(4, TILES)
+        load_g_codes(0, GROUPS, 4, 6)
+        load_density(1, 1)
+        load_density(2, 1)
+        load_g_codes(0, GROUPS, 6, 8)
+        load_density(3, 1)
+        load_field(0, 4)
+        load_field(4, 8)
+        load_g_codes(0, GROUPS, 8, TILES)
+        load_field(8, TILES)
+
+        for half in range(HALVES):
+            nc.tensor.matmul(
+                out=gain_bank[:, cols(half)], lhsT=ones[:], rhs=gain_row[:, cols(half)], start=True, stop=True
+            )
+
+        for g in range(GROUPS):
+            weigh(g, 0)
+            if g == GROUPS - 1:
+                nc.scalar.copy(out=gain_all[:], in_=gain_bank)
+            pack_scalar(g, 0)
+            if g > 0:
+                quantise_a(g - 1, 0)
+            pack_vector(g, 0)
+        quantise_a(GROUPS - 1, 0)
+        by_group(range(4), (0, 1))
+        by_sum(range(4), (2, 3))
+
+        weigh(0, 1)
+        pack_scalar(0, 1)
+        apply_gain(0)
+        pack_vector(0, 1)
+        apply_gain(1, 2)
+        quantise_a(0, 1)
+        apply_gain(3)
+        by_sum((4, 5))
+        by_group(range(8, 12), (0,))
+        by_sum((6, 7))
+        for g in (1, 2):
+            weigh(g, 1)
+            pack_scalar(g, 1)
+            pack_vector(g, 1)
+        quantise_a(1, 1)
+        weigh(3, 1)
+        pack_scalar(3, 1)
+        apply_gain(4, 5)
+        pack_vector(3, 1)
+        quantise_a(2, 1)
+        quantise_a(3, 1)
+        by_group(range(8, 12), (1,))
+        by_group((12, 13), (0, 1))
+        by_sum(range(8, 14), (2, 3))
+
+        for tile in (0, 1):
+            add_field(nc.vector, tile, 0, N)
+            round_y(tile, 0, N)
+        apply_gain(*range(6, 12))
+        add_field(nc.gpsimd, 6, 0, N)
+        add_field(nc.gpsimd, 0, N, C)
+        by_sum((14, 15))
+        add_field(nc.vector, 1, N, C)
+        for tile in (0, 1):
+            round_y(tile, N, C)
+        for tile in (2, 3):
+            add_field(nc.vector, tile)
+            round_y(tile)
+        turn(0, 1)
+        by_sum((16, 17))
+        unload(0, 1)
+        turn(2, 3)
+        store_y(0, 2)
+        store_y(2, 4)
+
+        apply_gain(*range(12, 16))
+        add_field(nc.gpsimd, 4, GPSIMD_FROM, C)
+        by_sum((18, 19))
+        add_field(nc.vector, 4, 0, GPSIMD_FROM)
+        add_field(nc.vector, 5)
+        add_field(nc.vector, 6, N, C)
+        add_field(nc.vector, 7)
+        round_y(4)
+        round_y(5)
+        unload(2, 3)
+        round_y(6)
+        round_y(7)
+        turn(4, 5)
+        by_sum((20, 21))
+        unload(4, 5)
+        turn(6, 7)
+        unload(6, 7)
+        store_y(4, 6)
+        store_y(6, 8)
+
+        apply_gain(*range(16, 20))
+        add_field(nc.gpsimd, 8, 0, N)
+        by_sum((22, 23))
+        add_field(nc.vector, 8, N, C)
+        for half in range(HALVES):
+            quantise_y(half, 0, 4)
+        add_field(nc.vector, 9)
+        round_y(8)
+        round_y(9)
+        turn(8, 9)
+        unload(8, 9)
+        store_codes(0, 4)
+        store_y(8, 10)
+
+        last = TILES - 1
+        apply_gain(20, 21, 22)
+        add_field(nc.gpsimd, last - 1, 0, N)
+        add_field(nc.vector, last - 1, N, C)
+        add_field(nc.vector, last, 0, N)
+        for half in range(HALVES):
+            quantise_y(half, 4, 8)
+        round_y(last - 1)
+        round_y(last, 0, N)
+        turn(10, 11)
+        unload(10)
+        apply_gain(23)
+        quantise_y(0, 8, 10)
+        nc.vector.tensor_tensor(
+            out=rounded[:, last % ROUNDED_BUFS, :, N // PACK :],
+            in0=by_pairs(y[:, last, N:]),
+            in1=by_pairs(field_sb[:, last, N:]),
+            op=ADD,
+        )
+        quantise_y(1, 8, 10)
+        add_field(nc.vector, last, N, C)
+        turn(12)
+        unload(11, 12)
+        quantise_y(1, last - 1, last)
+        quantise_y(0, last - 1, TILES)
+        quantise_y(1, last, TILES)
+        store_y(last - 1, last)
+        store_y(last, TILES, 0, N)
+        store_codes(4, 8)
+        store_bytes(nc.sync, range(QUADRANTS), 0, 8)
+        store_y(last, TILES, N, C)
+        store_codes(8, 10)
+        store_bytes(nc.sync, (0, 1), 8, TILES)
+        store_bytes(nc.scalar, (2, 3), 8, TILES)
+        store_codes(10, TILES)

@@ -25,15 +25,16 @@ TILES = R // P
 QUADRANTS = 4
 
 BANKS = 8
-FIRST_SUMS = [(tile, half) for half in range(HALVES) for tile in range(BANKS)]
-SUMS = FIRST_SUMS + [(tile, half) for tile in range(BANKS, TILES) for half in range(HALVES)]
 SUM_BANKS = 6
 TURNS = [(tile, 0, C) for tile in range(TILES - 1)] + [(TILES - 1, 0, N), (TILES - 1, N, C)]
+DENSITY_LOADS = [(0, 0, N), (0, N, C), (1, 0, C), (2, 0, C), (3, 0, N), (3, N, C)]
+G_CODE_LOADS = [(0, 2, 0, 4), (2, 4, 0, 2), (2, 4, 2, 4), (0, 4, 4, 6), (0, 4, 6, 8), (0, 4, 8, 12)]
+G_BYTE_BLOCKS = [(0, 4), (4, 12)]
+Y_CODE_BLOCKS = [(0, 4), (4, 8), (8, 10), (10, 12)]
+Y_BYTE_BLOCKS = [(0, 8), (8, 12)]
 ROUNDED_BUFS = 6
-CHUNK = 4
 
-VECTOR_COLS = (256, 160)
-GPSIMD_FROM = 384
+VECTOR_COLS = 224
 
 
 def tile_winding_dipole_sum_k2_kernel(
@@ -45,24 +46,41 @@ def tile_winding_dipole_sum_k2_kernel(
         psum = ctx.enter_context(tc.psum_pool(name="psum", bufs=1))
         ctx.enter_context(tc.manual_schedule())
 
+        def blocks(name, bounds, depth, dtype, inner=()):
+            return {
+                (b0, b1): sbuf.tile([P, depth, (b1 - b0) * P, *inner], dtype, name="%s%d" % (name, b0), align_bytes=64)
+                for b0, b1 in bounds
+            }
+
+        def window(tiles, index, tile0, tile1):
+            b0, b1 = [b for b in tiles if b[0] <= tile0 < b[1]][0]
+            return tiles[b0, b1][:, index, (tile0 - b0) * P : (tile1 - b0) * P]
+
         area = sbuf.tile([P, GROUPS, 16], BF16)
         gain_row = sbuf.tile([P, C], BF16)
         gain_all = sbuf.tile([P, C], BF16)
         ones_f32 = sbuf.tile([P, P], F32)
         ones = sbuf.tile([P, P], BF16)
         ident = sbuf.tile([P, P], F32)
-        g_codes = sbuf.tile([P, GROUPS, R], U32, align_bytes=64)
-        g_bytes = sbuf.tile([P, GROUPS, R], U8, align_bytes=64)
-        rows = sbuf.tile([P, GROUPS, PACK, C], BF16, align_bytes=64)
+        g_codes = {
+            (g0, g1, b0, b1): sbuf.tile([P, g1 - g0, (b1 - b0) * P], U32, name="g_codes%d" % i, align_bytes=64)
+            for i, (g0, g1, b0, b1) in enumerate(G_CODE_LOADS)
+        }
+        g_bytes = blocks("g_bytes", G_BYTE_BLOCKS, GROUPS, U8)
+        rows = {
+            (g, c0, c1): sbuf.tile([P, PACK, c1 - c0], BF16, name="rows%d" % i, align_bytes=64)
+            for i, (g, c0, c1) in enumerate(DENSITY_LOADS)
+        }
         packed = sbuf.tile([P, 2, C, PACK], BF16, align_bytes=64)
         a_codes = sbuf.tile([P, GROUPS, C], U32, align_bytes=64)
         a_bytes = sbuf.tile([P, GROUPS, C], U8, align_bytes=64)
         field_sb = sbuf.tile([P, TILES, C], BF16, align_bytes=64)
         y = sbuf.tile([P, TILES, C], F32, align_bytes=64)
         rounded = sbuf.tile([P, ROUNDED_BUFS, 2, C // PACK, 2], BF16, align_bytes=64)
-        turned = sbuf.tile([P, 2, HALVES, CHUNK * P, PACK], BF16, align_bytes=64)
-        y_codes = sbuf.tile([P, HALVES, R], U32, align_bytes=64)
-        y_bytes = sbuf.tile([P, HALVES, R], U8, align_bytes=64)
+        rounded_last = sbuf.tile([P, 2, P, 2], BF16, align_bytes=64)
+        turned = blocks("turned", Y_CODE_BLOCKS, HALVES, BF16, (PACK,))
+        y_codes = blocks("y_codes", Y_CODE_BLOCKS, HALVES, U32)
+        y_bytes = blocks("y_bytes", Y_BYTE_BLOCKS, HALVES, U8)
         banks = [psum.tile([P, N], F32, name="bank%d" % i) for i in range(BANKS)]
         gain_bank = banks[BANKS - 1][:].bitcast(BF16)
 
@@ -78,41 +96,39 @@ def tile_winding_dipole_sum_k2_kernel(
         def turn_bank(i):
             return banks[SUM_BANKS + i % 2][:, : (TURNS[i][2] - TURNS[i][1]) // 2]
 
-        def load_density(g, half):
-            src = density[span(g, g + 1, P * PACK), cols(half)]
-            nc.sync.dma_start(out=rows[:, g, :, cols(half)], in_=src.rearrange("(p t) c -> p t c", t=PACK))
+        def load_density(g, c0=0, c1=C):
+            src = density[span(g, g + 1, P * PACK), c0:c1]
+            nc.sync.dma_start(out=rows[g, c0, c1][:], in_=src.rearrange("(p t) c -> p t c", t=PACK))
 
         def load_g_codes(g0, g1, tile0, tile1):
             src = g_words.rearrange("g p r t -> p g (r t)")[:, g0:g1, span(tile0, tile1, P * PACK)]
-            nc.sync.dma_start(out=g_codes[:, g0:g1, span(tile0, tile1)].bitcast(I32), in_=src.bitcast(I32))
+            nc.sync.dma_start(out=g_codes[g0, g1, tile0, tile1][:].bitcast(I32), in_=src.bitcast(I32))
 
         def load_g_bytes(tile0, tile1):
             for q in range(QUADRANTS):
                 src = g_scales[:, 4 * q : 4 * q + 4, span(tile0, tile1)].rearrange("g j r -> j g r")
-                nc.sync.dma_start(
-                    out=g_bytes[32 * q : 32 * q + 4, :, span(tile0, tile1)].bitcast(I32), in_=src.bitcast(I32)
-                )
+                nc.sync.dma_start(out=g_bytes[tile0, tile1][32 * q : 32 * q + 4].bitcast(I32), in_=src.bitcast(I32))
 
         def load_field(tile0, tile1):
             src = field[span(tile0, tile1), :].rearrange("(a p) c -> p a c", p=P)
             nc.sync.dma_start(out=field_sb[:, tile0:tile1], in_=src)
 
-        def weigh(g, half):
+        def weigh(g, c0=0, c1=C):
             for t in range(PACK):
-                row = rows[:, g, t, cols(half)]
+                row = rows[g, c0, c1][:, t]
                 nc.vector.tensor_scalar(out=row, in0=row, scalar1=area[:, g, t : t + 1], scalar2=None, op0=MULT)
 
-        def pack_views(g, c0, c1):
-            dst = packed[:, g % 2, c0:c1].rearrange("p (c i) t -> p c t i", i=4)
-            src = rows[:, g, :, c0:c1].rearrange("p t (c i) -> p c t i", i=4)
+        def pack_views(g, half, c0, c1):
+            dst = packed[:, g % 2, half * N + c0 : half * N + c1].rearrange("p (c i) t -> p c t i", i=4)
+            load = [d for d in DENSITY_LOADS if d[0] == g and d[1] <= half * N < d[2]][0]
+            first = half * N - load[1]
+            src = rows[load][:, :, first + c0 : first + c1].rearrange("p t (c i) -> p c t i", i=4)
             return dst, src
 
-        def pack_vector(g, half):
-            dst, src = pack_views(g, half * N, half * N + VECTOR_COLS[half])
+        def pack(g, half):
+            dst, src = pack_views(g, half, 0, VECTOR_COLS)
             nc.vector.tensor_copy(out=dst, in_=src)
-
-        def pack_scalar(g, half):
-            dst, src = pack_views(g, half * N + VECTOR_COLS[half], (half + 1) * N)
+            dst, src = pack_views(g, half, VECTOR_COLS, N)
             nc.scalar.copy(out=dst, in_=src)
 
         def quantise_a(g, half):
@@ -123,11 +139,12 @@ def tile_winding_dipole_sum_k2_kernel(
             )
 
         def mx_pass(n, g):
-            tile, half = SUMS[n]
+            tile, half = divmod(n, HALVES)
+            g0, g1, b0, b1 = [d for d in G_CODE_LOADS if d[0] <= g < d[1] and d[2] <= tile < d[3]][0]
             nc.tensor.matmul_mx(
                 out=sum_bank(n),
-                lhsT=g_codes[:, g, span(tile, tile + 1)].bitcast(E5M2),
-                lhsT_scale=g_bytes[:, g, span(tile, tile + 1)],
+                lhsT=g_codes[g0, g1, b0, b1][:, g - g0, span(tile - b0, tile - b0 + 1)].bitcast(E5M2),
+                lhsT_scale=window(g_bytes, g, tile, tile + 1),
                 rhs=a_codes[:, g, cols(half)].bitcast(E4M3),
                 rhs_scale=a_bytes[:, g, cols(half)],
                 start=(g == 0),
@@ -139,14 +156,14 @@ def tile_winding_dipole_sum_k2_kernel(
                 for n in sums:
                     mx_pass(n, g)
 
-        def by_sum(sums, groups=range(GROUPS)):
+        def by_sum(*sums):
             for n in sums:
-                for g in groups:
+                for g in range(GROUPS):
                     mx_pass(n, g)
 
         def apply_gain(*sums):
             for n in sums:
-                tile, half = SUMS[n]
+                tile, half = divmod(n, HALVES)
                 nc.vector.tensor_tensor(
                     out=y[:, tile, cols(half)], in0=sum_bank(n), in1=gain_all[:, cols(half)], op=MULT
                 )
@@ -166,25 +183,24 @@ def tile_winding_dipole_sum_k2_kernel(
             for i in turns:
                 tile, c0, c1 = TURNS[i]
                 bank = turn_bank(i).rearrange("p (h u r) -> p h u r", u=2, r=P)
-                words = rounded[:, tile % ROUNDED_BUFS].rearrange("r u w e -> r u (w e)").bitcast(F32)
-                for half in range(c0 // N, c1 // N):
+                src = rounded_last[:] if c0 > 0 else rounded[:, tile % ROUNDED_BUFS]
+                words = src.rearrange("r u w e -> r u (w e)").bitcast(F32)
+                for j in range((c1 - c0) // N):
                     for u in range(2):
-                        nc.tensor.transpose(bank[:, half - c0 // N, u], words[:, u, span(half, half + 1)], ident[:])
+                        nc.tensor.transpose(bank[:, j, u], words[:, u, span(j, j + 1)], ident[:])
 
         def unload(*turns):
             for i in turns:
                 tile, c0, c1 = TURNS[i]
-                place = span(tile % CHUNK, tile % CHUNK + 1)
-                dst = turned[:, (tile // CHUNK) % 2, c0 // N : c1 // N, place]
+                dst = window(turned, slice(c0 // N, c1 // N), tile, tile + 1)
                 dst = dst.rearrange("p h r t -> p h (r t)").bitcast(F32).rearrange("p h (r u) -> p h r u", u=2)
                 nc.scalar.copy(out=dst, in_=turn_bank(i).rearrange("p (h u r) -> p h r u", u=2, r=P))
 
         def quantise_y(half, tile0, tile1):
-            place = span(tile0 % CHUNK, tile0 % CHUNK + tile1 - tile0)
             nc.vector.quantize_mx(
-                out=y_codes[:, half, span(tile0, tile1)].bitcast(E4M3),
-                scales=y_bytes[:, half, span(tile0, tile1)],
-                in_=turned[:, (tile0 // CHUNK) % 2, half, place].rearrange("p r t -> p (r t)"),
+                out=window(y_codes, half, tile0, tile1).bitcast(E4M3),
+                scales=window(y_bytes, half, tile0, tile1),
+                in_=window(turned, half, tile0, tile1).rearrange("p r t -> p (r t)"),
             )
 
         def store_y(tile0, tile1, c0=0, c1=C):
@@ -193,41 +209,40 @@ def tile_winding_dipole_sum_k2_kernel(
 
         def store_codes(tile0, tile1):
             dst = out_1.rearrange("h p r t -> p h (r t)")[:, :, span(tile0, tile1, P * PACK)]
-            nc.sync.dma_start(out=dst.bitcast(I32), in_=y_codes[:, :, span(tile0, tile1)].bitcast(I32))
+            nc.sync.dma_start(out=dst.bitcast(I32), in_=y_codes[tile0, tile1][:].bitcast(I32))
 
         def store_bytes(engine, quadrants, tile0, tile1):
             for q in quadrants:
                 dst = out_2[:, 4 * q : 4 * q + 4, span(tile0, tile1)].rearrange("h j r -> j h r")
-                engine.dma_start(
-                    out=dst.bitcast(I32), in_=y_bytes[32 * q : 32 * q + 4, :, span(tile0, tile1)].bitcast(I32)
-                )
+                engine.dma_start(out=dst.bitcast(I32), in_=y_bytes[tile0, tile1][32 * q : 32 * q + 4].bitcast(I32))
 
 
         nc.vector.memset(ones_f32[:], 1.0)
         nc.vector.memset(gain_row[:], 0.0)
-        nc.vector.memset(g_bytes[:].rearrange("p g r -> p (g r)").bitcast(U32), 0)
+        for block in G_BYTE_BLOCKS:
+            nc.vector.memset(g_bytes[block][:].rearrange("p g r -> p (g r)").bitcast(U32), 0)
         make_identity(nc, ident[:])
         area_src = area_weight.rearrange("(g p t) -> p g t", p=P, t=PACK)
         nc.scalar.dma_start(out=area[:, :1, :PACK], in_=area_src[:, :1])
         nc.scalar.dma_start(out=area[:, 1:, :PACK], in_=area_src[:, 1:])
         nc.scalar.copy(out=ones[:], in_=ones_f32[:])
 
-        load_density(0, 0)
-        load_density(1, 0)
+        load_density(0, 0, N)
+        load_density(0, N, C)
+        load_density(1)
+        load_density(2)
         load_g_bytes(0, 4)
-        load_density(2, 0)
         nc.sync.dma_start(out=gain_row[0:1, :], in_=gain.rearrange("(o c) -> o c", o=1))
-        load_density(3, 0)
         load_g_codes(0, 2, 0, 4)
-        load_g_codes(2, 4, 0, 4)
-        load_density(0, 1)
+        load_density(3, 0, N)
+        load_g_codes(2, 4, 0, 2)
+        load_density(3, N, C)
+        load_g_codes(2, 4, 2, 4)
+        load_field(0, 2)
         load_g_bytes(4, TILES)
         load_g_codes(0, GROUPS, 4, 6)
-        load_density(1, 1)
-        load_density(2, 1)
+        load_field(2, 4)
         load_g_codes(0, GROUPS, 6, 8)
-        load_density(3, 1)
-        load_field(0, 4)
         load_field(4, 8)
         load_g_codes(0, GROUPS, 8, TILES)
         load_field(8, TILES)
@@ -237,104 +252,63 @@ def tile_winding_dipole_sum_k2_kernel(
                 out=gain_bank[:, cols(half)], lhsT=ones[:], rhs=gain_row[:, cols(half)], start=True, stop=True
             )
 
-        for g in range(GROUPS):
-            weigh(g, 0)
-            if g == GROUPS - 1:
-                nc.scalar.copy(out=gain_all[:], in_=gain_bank)
-            pack_scalar(g, 0)
-            if g > 0:
-                quantise_a(g - 1, 0)
-            pack_vector(g, 0)
-        quantise_a(GROUPS - 1, 0)
-        by_group(range(4), (0, 1))
-        by_sum(range(4), (2, 3))
-
-        weigh(0, 1)
-        pack_scalar(0, 1)
-        apply_gain(0)
-        pack_vector(0, 1)
-        apply_gain(1, 2)
-        quantise_a(0, 1)
-        apply_gain(3)
-        by_sum((4, 5))
-        by_group(range(8, 12), (0,))
-        by_sum((6, 7))
+        weigh(0, 0, N)
+        pack(0, 0)
+        weigh(0, N, C)
+        quantise_a(0, 0)
+        pack(0, 1)
         for g in (1, 2):
-            weigh(g, 1)
-            pack_scalar(g, 1)
-            pack_vector(g, 1)
-        quantise_a(1, 1)
-        weigh(3, 1)
-        pack_scalar(3, 1)
-        apply_gain(4, 5)
-        pack_vector(3, 1)
+            weigh(g)
+            quantise_a(g - 1, 1)
+            pack(g, 0)
+            pack(g, 1)
+            quantise_a(g, 0)
+        nc.scalar.copy(out=gain_all[:], in_=gain_bank)
+        weigh(3, 0, N)
         quantise_a(2, 1)
+        pack(3, 0)
+        weigh(3, N, C)
+        quantise_a(3, 0)
+        pack(3, 1)
         quantise_a(3, 1)
-        by_group(range(8, 12), (1,))
-        by_group((12, 13), (0, 1))
-        by_sum(range(8, 14), (2, 3))
 
-        for tile in (0, 1):
-            add_field(nc.vector, tile, 0, N)
-            round_y(tile, 0, N)
-        apply_gain(*range(6, 12))
-        add_field(nc.gpsimd, 6, 0, N)
-        add_field(nc.gpsimd, 0, N, C)
-        by_sum((14, 15))
-        add_field(nc.vector, 1, N, C)
-        for tile in (0, 1):
-            round_y(tile, N, C)
-        for tile in (2, 3):
-            add_field(nc.vector, tile)
+        early, late = (0, 2, 1, 3), (4, 6, 5, 7)
+        by_group(early, (0, 1))
+        by_group(late, (0,))
+        by_group(early, (2,))
+        by_group(late, (1,))
+        by_group(early, (3,))
+        by_group(late, (2, 3))
+
+        sums_before = {4: (12, 13, 14)}
+        sums_after = {0: (8, 9, 10, 11), 4: (15, 16, 17), 6: (18, 19, 20), 8: (21, 22, 23)}
+        for tile in range(0, TILES - 2, 2):
+            behind = (tile - 2, tile - 1) if tile > 0 else ()
+            apply_gain(*(early if tile == 0 else range(2 * tile, 2 * tile + 4)))
+            by_sum(*sums_before.get(tile, ()))
+            turn(*behind)
+            add_field(nc.gpsimd, tile, 0, N)
+            add_field(nc.vector, tile, N, C)
+            add_field(nc.vector, tile + 1)
+            unload(*behind)
             round_y(tile)
-        turn(0, 1)
-        by_sum((16, 17))
-        unload(0, 1)
-        turn(2, 3)
-        store_y(0, 2)
-        store_y(2, 4)
-
-        apply_gain(*range(12, 16))
-        add_field(nc.gpsimd, 4, GPSIMD_FROM, C)
-        by_sum((18, 19))
-        add_field(nc.vector, 4, 0, GPSIMD_FROM)
-        add_field(nc.vector, 5)
-        add_field(nc.vector, 6, N, C)
-        add_field(nc.vector, 7)
-        round_y(4)
-        round_y(5)
-        unload(2, 3)
-        round_y(6)
-        round_y(7)
-        turn(4, 5)
-        by_sum((20, 21))
-        unload(4, 5)
-        turn(6, 7)
-        unload(6, 7)
-        store_y(4, 6)
-        store_y(6, 8)
-
-        apply_gain(*range(16, 20))
-        add_field(nc.gpsimd, 8, 0, N)
-        by_sum((22, 23))
-        add_field(nc.vector, 8, N, C)
+            round_y(tile + 1)
+            by_sum(*sums_after.get(tile, ()))
+            if tile == 6:
+                for half in range(HALVES):
+                    quantise_y(half, 0, 4)
+                store_codes(0, 4)
+            store_y(tile, tile + 2)
         for half in range(HALVES):
-            quantise_y(half, 0, 4)
-        add_field(nc.vector, 9)
-        round_y(8)
-        round_y(9)
+            quantise_y(half, 4, 8)
         turn(8, 9)
         unload(8, 9)
-        store_codes(0, 4)
-        store_y(8, 10)
 
         last = TILES - 1
         apply_gain(20, 21, 22)
         add_field(nc.gpsimd, last - 1, 0, N)
         add_field(nc.vector, last - 1, N, C)
         add_field(nc.vector, last, 0, N)
-        for half in range(HALVES):
-            quantise_y(half, 4, 8)
         round_y(last - 1)
         round_y(last, 0, N)
         turn(10, 11)
@@ -342,7 +316,7 @@ def tile_winding_dipole_sum_k2_kernel(
         apply_gain(23)
         quantise_y(0, 8, 10)
         nc.vector.tensor_tensor(
-            out=rounded[:, last % ROUNDED_BUFS, :, N // PACK :],
+            out=rounded_last[:],
             in0=by_pairs(y[:, last, N:]),
             in1=by_pairs(field_sb[:, last, N:]),
             op=ADD,
@@ -354,12 +328,12 @@ def tile_winding_dipole_sum_k2_kernel(
         quantise_y(1, last - 1, last)
         quantise_y(0, last - 1, TILES)
         quantise_y(1, last, TILES)
+        store_bytes(nc.sync, range(QUADRANTS), 0, 8)
+        store_codes(4, 8)
         store_y(last - 1, last)
         store_y(last, TILES, 0, N)
-        store_codes(4, 8)
-        store_bytes(nc.sync, range(QUADRANTS), 0, 8)
-        store_y(last, TILES, N, C)
         store_codes(8, 10)
+        store_y(last, TILES, N, C)
         store_bytes(nc.sync, (0, 1), 8, TILES)
         store_bytes(nc.scalar, (2, 3), 8, TILES)
         store_codes(10, TILES)

from contextlib import ExitStack

import concourse.mybir as mybir
from concourse.masks import make_identity

F32 = mybir.dt.float32
BF16 = mybir.dt.bfloat16
I32 = mybir.dt.int32
U32 = mybir.dt.uint32
U8 = mybir.dt.uint8
E4M3 = mybir.dt.float8_e4m3fn_x4
E5M2 = mybir.dt.float8_e5m2_x4
MULT = mybir.AluOpType.mult
ADD = mybir.AluOpType.add

R, K, C = 1536, 2048, 1024
FLOPS = 2 * R * K * C

P = 128
PACK = 4
N = 512
GROUPS = K // (P * PACK)
HALVES = C // N
TILES = R // P
QUADRANTS = 4

BANKS = 8
SUM_BANKS = 6
TURNS = [(tile, 0, C) for tile in range(TILES - 1)] + [(TILES - 1, 0, N), (TILES - 1, N, C)]
DENSITY_LOADS = [(0, 0, N), (0, N, C), (1, 0, C), (2, 0, C), (3, 0, N), (3, N, C)]
G_CODE_LOADS = [(0, 2, 0, 4), (2, 4, 0, 2), (2, 4, 2, 4), (0, 4, 4, 6), (0, 4, 6, 8), (0, 4, 8, 12)]
G_BYTE_BLOCKS = [(0, 4), (4, 12)]
Y_CODE_BLOCKS = [(0, 4), (4, 8), (8, 10), (10, 12)]
Y_BYTE_BLOCKS = [(0, 8), (8, 12)]
ROUNDED_BUFS = 6

VECTOR_COLS = 224


def tile_winding_dipole_sum_k2_kernel(
    tc, g_words, g_scales, density, area_weight, gain, field, out_0, out_1, out_2
):
    nc = tc.nc
    with ExitStack() as ctx:
        sbuf = ctx.enter_context(tc.tile_pool(name="sbuf", bufs=1))
        psum = ctx.enter_context(tc.psum_pool(name="psum", bufs=1))
        ctx.enter_context(tc.manual_schedule())

        def blocks(name, bounds, depth, dtype, inner=()):
            return {
                (b0, b1): sbuf.tile([P, depth, (b1 - b0) * P, *inner], dtype, name="%s%d" % (name, b0), align_bytes=64)
                for b0, b1 in bounds
            }

        def window(tiles, index, tile0, tile1):
            b0, b1 = [b for b in tiles if b[0] <= tile0 < b[1]][0]
            return tiles[b0, b1][:, index, (tile0 - b0) * P : (tile1 - b0) * P]

        area = sbuf.tile([P, GROUPS, 16], BF16)
        gain_row = sbuf.tile([P, C], BF16)
        gain_all = sbuf.tile([P, C], BF16)
        ones_f32 = sbuf.tile([P, P], F32)
        ones = sbuf.tile([P, P], BF16)
        ident = sbuf.tile([P, P], F32)
        g_codes = {
            (g0, g1, b0, b1): sbuf.tile([P, g1 - g0, (b1 - b0) * P], U32, name="g_codes%d" % i, align_bytes=64)
            for i, (g0, g1, b0, b1) in enumerate(G_CODE_LOADS)
        }
        g_bytes = blocks("g_bytes", G_BYTE_BLOCKS, GROUPS, U8)
        rows = {
            (g, c0, c1): sbuf.tile([P, PACK, c1 - c0], BF16, name="rows%d" % i, align_bytes=64)
            for i, (g, c0, c1) in enumerate(DENSITY_LOADS)
        }
        packed = sbuf.tile([P, 2, C, PACK], BF16, align_bytes=64)
        a_codes = sbuf.tile([P, GROUPS, C], U32, align_bytes=64)
        a_bytes = sbuf.tile([P, GROUPS, C], U8, align_bytes=64)
        field_sb = sbuf.tile([P, TILES, C], BF16, align_bytes=64)
        y = sbuf.tile([P, TILES, C], F32, align_bytes=64)
        rounded = sbuf.tile([P, ROUNDED_BUFS, 2, C // PACK, 2], BF16, align_bytes=64)
        rounded_last = sbuf.tile([P, 2, P, 2], BF16, align_bytes=64)
        turned = blocks("turned", Y_CODE_BLOCKS, HALVES, BF16, (PACK,))
        y_codes = blocks("y_codes", Y_CODE_BLOCKS, HALVES, U32)
        y_bytes = blocks("y_bytes", Y_BYTE_BLOCKS, HALVES, U8)
        banks = [psum.tile([P, N], F32, name="bank%d" % i) for i in range(BANKS)]
        gain_bank = banks[BANKS - 1][:].bitcast(BF16)

        def cols(half):
            return slice(half * N, (half + 1) * N)

        def span(first, end, width=P):
            return slice(first * width, end * width)

        def sum_bank(n):
            return banks[n if n < BANKS else (n - BANKS) % SUM_BANKS][:]

        def turn_bank(i):
            return banks[SUM_BANKS + i % 2][:, : (TURNS[i][2] - TURNS[i][1]) // 2]

        def load_density(g, c0=0, c1=C):
            src = density[span(g, g + 1, P * PACK), c0:c1]
            nc.sync.dma_start(out=rows[g, c0, c1][:], in_=src.rearrange("(p t) c -> p t c", t=PACK))

        def load_g_codes(g0, g1, tile0, tile1):
            src = g_words.rearrange("g p r t -> p g (r t)")[:, g0:g1, span(tile0, tile1, P * PACK)]
            nc.sync.dma_start(out=g_codes[g0, g1, tile0, tile1][:].bitcast(I32), in_=src.bitcast(I32))

        def load_g_bytes(tile0, tile1):
            for q in range(QUADRANTS):
                src = g_scales[:, 4 * q : 4 * q + 4, span(tile0, tile1)].rearrange("g j r -> j g r")
                nc.sync.dma_start(out=g_bytes[tile0, tile1][32 * q : 32 * q + 4].bitcast(I32), in_=src.bitcast(I32))

        def load_field(tile0, tile1):
            src = field[span(tile0, tile1), :].rearrange("(a p) c -> p a c", p=P)
            nc.sync.dma_start(out=field_sb[:, tile0:tile1], in_=src)

        def weigh(g, c0=0, c1=C):
            for t in range(PACK):
                row = rows[g, c0, c1][:, t]
                nc.vector.tensor_scalar(out=row, in0=row, scalar1=area[:, g, t : t + 1], scalar2=None, op0=MULT)

        def pack_views(g, half, c0, c1):
            dst = packed[:, g % 2, half * N + c0 : half * N + c1].rearrange("p (c i) t -> p c t i", i=4)
            load = [d for d in DENSITY_LOADS if d[0] == g and d[1] <= half * N < d[2]][0]
            first = half * N - load[1]
            src = rows[load][:, :, first + c0 : first + c1].rearrange("p t (c i) -> p c t i", i=4)
            return dst, src

        def pack(g, half):
            dst, src = pack_views(g, half, 0, VECTOR_COLS)
            nc.vector.tensor_copy(out=dst, in_=src)
            dst, src = pack_views(g, half, VECTOR_COLS, N)
            nc.scalar.copy(out=dst, in_=src)

        def quantise_a(g, half):
            nc.vector.quantize_mx(
                out=a_codes[:, g, cols(half)].bitcast(E4M3),
                scales=a_bytes[:, g, cols(half)],
                in_=packed[:, g % 2, cols(half)].rearrange("p c t -> p (c t)"),
            )

        def mx_pass(n, g):
            tile, half = divmod(n, HALVES)
            g0, g1, b0, b1 = [d for d in G_CODE_LOADS if d[0] <= g < d[1] and d[2] <= tile < d[3]][0]
            nc.tensor.matmul_mx(
                out=sum_bank(n),
                lhsT=g_codes[g0, g1, b0, b1][:, g - g0, span(tile - b0, tile - b0 + 1)].bitcast(E5M2),
                lhsT_scale=window(g_bytes, g, tile, tile + 1),
                rhs=a_codes[:, g, cols(half)].bitcast(E4M3),
                rhs_scale=a_bytes[:, g, cols(half)],
                start=(g == 0),
                stop=(g == GROUPS - 1),
            )

        def by_group(sums, groups):
            for g in groups:
                for n in sums:
                    mx_pass(n, g)

        def by_sum(*sums):
            for n in sums:
                for g in range(GROUPS):
                    mx_pass(n, g)

        def apply_gain(*sums):
            for n in sums:
                tile, half = divmod(n, HALVES)
                nc.vector.tensor_tensor(
                    out=y[:, tile, cols(half)], in0=sum_bank(n), in1=gain_all[:, cols(half)], op=MULT
                )

        def add_field(engine, tile, c0=0, c1=C):
            part = y[:, tile, c0:c1]
            engine.tensor_tensor(out=part, in0=part, in1=field_sb[:, tile, c0:c1], op=ADD)

        def by_pairs(ap):
            return ap.rearrange("r (w u e) -> r u w e", u=2, e=2)

        def round_y(tile, c0=0, c1=C):
            dst = rounded[:, tile % ROUNDED_BUFS, :, c0 // PACK : c1 // PACK]
            nc.scalar.copy(out=dst, in_=by_pairs(y[:, tile, c0:c1]))

        def turn(*turns):
            for i in turns:
                tile, c0, c1 = TURNS[i]
                bank = turn_bank(i).rearrange("p (h u r) -> p h u r", u=2, r=P)
                src = rounded_last[:] if c0 > 0 else rounded[:, tile % ROUNDED_BUFS]
                words = src.rearrange("r u w e -> r u (w e)").bitcast(F32)
                for j in range((c1 - c0) // N):
                    for u in range(2):
                        nc.tensor.transpose(bank[:, j, u], words[:, u, span(j, j + 1)], ident[:])

        def unload(*turns):
            for i in turns:
                tile, c0, c1 = TURNS[i]
                dst = window(turned, slice(c0 // N, c1 // N), tile, tile + 1)
                dst = dst.rearrange("p h r t -> p h (r t)").bitcast(F32).rearrange("p h (r u) -> p h r u", u=2)
                nc.scalar.copy(out=dst, in_=turn_bank(i).rearrange("p (h u r) -> p h r u", u=2, r=P))

        def quantise_y(half, tile0, tile1):
            nc.vector.quantize_mx(
                out=window(y_codes, half, tile0, tile1).bitcast(E4M3),
                scales=window(y_bytes, half, tile0, tile1),
                in_=window(turned, half, tile0, tile1).rearrange("p r t -> p (r t)"),
            )

        def store_y(tile0, tile1, c0=0, c1=C):
            dst = out_0[span(tile0, tile1), c0:c1].rearrange("(a p) c -> p a c", p=P)
            nc.sync.dma_start(out=dst, in_=y[:, tile0:tile1, c0:c1])

        def store_codes(tile0, tile1):
            dst = out_1.rearrange("h p r t -> p h (r t)")[:, :, span(tile0, tile1, P * PACK)]
            nc.sync.dma_start(out=dst.bitcast(I32), in_=y_codes[tile0, tile1][:].bitcast(I32))

        def store_bytes(engine, quadrants, tile0, tile1):
            for q in quadrants:
                dst = out_2[:, 4 * q : 4 * q + 4, span(tile0, tile1)].rearrange("h j r -> j h r")
                engine.dma_start(out=dst.bitcast(I32), in_=y_bytes[tile0, tile1][32 * q : 32 * q + 4].bitcast(I32))


        nc.vector.memset(ones_f32[:], 1.0)
        nc.vector.memset(gain_row[:], 0.0)
        for block in G_BYTE_BLOCKS:
            nc.vector.memset(g_bytes[block][:].rearrange("p g r -> p (g r)").bitcast(U32), 0)
        make_identity(nc, ident[:])
        area_src = area_weight.rearrange("(g p t) -> p g t", p=P, t=PACK)
        nc.scalar.dma_start(out=area[:, :1, :PACK], in_=area_src[:, :1])
        nc.scalar.dma_start(out=area[:, 1:, :PACK], in_=area_src[:, 1:])
        nc.scalar.copy(out=ones[:], in_=ones_f32[:])

        load_density(0, 0, N)
        load_density(0, N, C)
        load_density(1)
        load_density(2)
        load_g_bytes(0, 4)
        nc.sync.dma_start(out=gain_row[0:1, :], in_=gain.rearrange("(o c) -> o c", o=1))
        load_g_codes(0, 2, 0, 4)
        load_density(3, 0, N)
        load_g_codes(2, 4, 0, 2)
        load_density(3, N, C)
        load_g_codes(2, 4, 2, 4)
        load_field(0, 2)
        load_g_bytes(4, TILES)
        load_g_codes(0, GROUPS, 4, 6)
        load_field(2, 4)
        load_g_codes(0, GROUPS, 6, 8)
        load_field(4, 8)
        load_g_codes(0, GROUPS, 8, TILES)
        load_field(8, TILES)

        for half in range(HALVES):
            nc.tensor.matmul(
                out=gain_bank[:, cols(half)], lhsT=ones[:], rhs=gain_row[:, cols(half)], start=True, stop=True
            )

        weigh(0, 0, N)
        pack(0, 0)
        weigh(0, N, C)
        quantise_a(0, 0)
        pack(0, 1)
        for g in (1, 2):
            weigh(g)
            quantise_a(g - 1, 1)
            pack(g, 0)
            pack(g, 1)
            quantise_a(g, 0)
        nc.scalar.copy(out=gain_all[:], in_=gain_bank)
        weigh(3, 0, N)
        quantise_a(2, 1)
        pack(3, 0)
        weigh(3, N, C)
        quantise_a(3, 0)
        pack(3, 1)
        quantise_a(3, 1)

        early, late = (0, 2, 1, 3), (4, 6, 5, 7)
        by_group(early, (0, 1))
        by_group(late, (0,))
        by_group(early, (2,))
        by_group(late, (1,))
        by_group(early, (3,))
        by_group(late, (2, 3))

        sums_before = {4: (12, 13, 14)}
        sums_after = {0: (8, 9, 10, 11), 4: (15, 16, 17), 6: (18, 19, 20), 8: (21, 22, 23)}
        for tile in range(0, TILES - 2, 2):
            behind = (tile - 2, tile - 1) if tile > 0 else ()
            apply_gain(*(early if tile == 0 else range(2 * tile, 2 * tile + 4)))
            by_sum(*sums_before.get(tile, ()))
            turn(*behind)
            add_field(nc.gpsimd, tile, 0, N)
            add_field(nc.vector, tile, N, C)
            add_field(nc.vector, tile + 1)
            unload(*behind)
            round_y(tile)
            round_y(tile + 1)
            by_sum(*sums_after.get(tile, ()))
            if tile == 6:
                for half in range(HALVES):
                    quantise_y(half, 0, 4)
                store_codes(0, 4)
            store_y(tile, tile + 2)
        for half in range(HALVES):
            quantise_y(half, 4, 8)
        turn(8, 9)
        unload(8, 9)

        last = TILES - 1
        apply_gain(20, 21, 22)
        add_field(nc.gpsimd, last - 1, 0, N)
        add_field(nc.vector, last - 1, N, C)
        add_field(nc.vector, last, 0, N)
        round_y(last - 1)
        round_y(last, 0, N)
        turn(10, 11)
        unload(10)
        apply_gain(23)
        quantise_y(0, 8, 10)
        nc.vector.tensor_tensor(
            out=rounded_last[:],
            in0=by_pairs(y[:, last, N:]),
            in1=by_pairs(field_sb[:, last, N:]),
            op=ADD,
        )
        quantise_y(1, 8, 10)
        add_field(nc.vector, last, N, C)
        turn(12)
        unload(11, 12)
        quantise_y(1, last - 1, last)
        quantise_y(0, last - 1, TILES)
        quantise_y(1, last, TILES)
        store_bytes(nc.sync, range(QUADRANTS), 0, 8)
        store_codes(4, 8)
        store_y(last - 1, last)
        store_y(last, TILES, 0, N)
        store_codes(8, 10)
        store_y(last, TILES, N, C)
        store_bytes(nc.sync, (0, 1), 8, TILES)
        store_bytes(nc.scalar, (2, 3), 8, TILES)
        store_codes(10, TILES)
